import numpy as np
import ml_dtypes


def mxq(x, axis, fmt="e4m3"):
    dtype, down = {"e4m3": (ml_dtypes.float8_e4m3fn, 7), "e5m2": (ml_dtypes.float8_e5m2, 14)}[fmt]
    v = np.moveaxis(np.asarray(x, np.float32).astype(ml_dtypes.bfloat16).astype(np.float64), axis, -1)
    blocks = v.reshape(v.shape[:-1] + (-1, 32))
    amax = np.abs(blocks).max(-1, keepdims=True)
    byte = np.maximum(np.where(amax > 0, np.frexp(amax)[1] - 1 + 127, 0) - down, 1)
    scale = np.exp2(byte - 127.0)
    codes = (blocks / scale).astype(np.float32).astype(dtype).astype(np.float64)
    return np.moveaxis((codes * scale).reshape(v.shape), -1, axis)


WIDE = False


def mx_kscale(k):
    if not WIDE:
        return np.ones(k)
    levels = np.array([10, -10, 5, -5, 0])
    if k % 512:
        return np.exp2(np.random.permutation(np.resize(levels, k // 32))).repeat(32)
    a = np.empty((k // 512, 16))
    for p in range(k // 512):
        a[p, :8] = np.random.permutation(np.resize(levels, 8))
        for g in range(8):
            far = levels[np.abs(levels - a[p, g]) >= 10]
            a[p, g + 8] = far[np.random.randint(len(far))]
    return np.exp2(a.ravel()).repeat(32)


BF16 = ml_dtypes.bfloat16


def bf(x):
    return np.asarray(x, np.float32).astype(BF16)


def f64(x):
    return np.asarray(x).astype(np.float64)

def planes(Y):
    n, m = Y.shape
    b = f64(bf(Y)).reshape(n // 32, 32, m)
    amax = np.abs(b).max(1)
    byte = np.clip(np.where(amax > 0, np.frexp(amax)[1] - 1 + 127 - 7, 1), 1, 254)
    codes = (b * np.exp2(127.0 - byte)[:, None, :]).reshape(n, m).astype(np.float32).astype(ml_dtypes.float8_e4m3fn).view(np.uint8)
    words = codes.reshape(n // 512, 128, 4, m).transpose(0, 1, 3, 2)
    return np.ascontiguousarray(words), np.ascontiguousarray(byte.astype(np.uint8).reshape(n // 512, 16, m))


C, P, N = 2, 256, 1024


def complex_mul(ar, ai, br, bi):
    return ar * br - ai * bi, ar * bi + ai * br


def scatter(arq, aiq, grq, giq):
    fr = (arq @ grq) - (aiq @ giq)
    fi = (arq @ giq) + (aiq @ grq)
    return fr, fi


def setup_inputs():
    s = mx_kscale(N)
    return {
        "u0": bf(np.random.standard_normal((C, P, N))),
        "v": bf(np.random.standard_normal((C, N)) * 0.7 * s),
        "g": bf(np.random.standard_normal((C, N, N)) / np.sqrt(N) / s[:, None]),
        "c": bf(np.random.standard_normal((C, N)) * 0.5),
    }


def core(u0, v, g, c):
    u0, v, g, c = f64(u0), f64(v), f64(g), f64(c)
    u0r, u0i = u0[0], u0[1]
    vr, vi = v[0][None, :], v[1][None, :]
    grq, giq = mxq(g[0], 0, "e4m3"), mxq(g[1], 0, "e4m3")
    cr, ci = c[0][None, :], c[1][None, :]

    ar, ai = complex_mul(vr, vi, u0r, u0i)
    fr, fi = scatter(mxq(ar, 1, "e4m3"), mxq(ai, 1, "e4m3"), grq, giq)
    dr, di = complex_mul(cr, ci, fr, fi)
    u1r = u0r + dr
    u1i = u0i + di

    a2r, a2i = complex_mul(vr, vi, u1r, u1i)
    f2r, f2i = scatter(mxq(a2r, 1, "e4m3"), mxq(a2i, 1, "e4m3"), grq, giq)
    resr = u1r - f2r - u0r
    resi = u1i - f2i - u0i
    d2r, d2i = complex_mul(cr, ci, resr, resi)
    u2r = u1r - d2r
    u2i = u1i - d2i

    return np.stack([u2r, u2i], axis=0)


def reference(u0, v, g, c):
    R_out = core(u0, v, g, c)
    words, scales = planes(np.moveaxis(R_out, 2, 0).reshape(1024, -1))
    return R_out, words, scales

@@ -1,0 +1,608 @@
+from contextlib import ExitStack
+
+import concourse.mybir as mybir
+from concourse.masks import make_identity
+
+F32 = mybir.dt.float32
+BF16 = mybir.dt.bfloat16
+U32 = mybir.dt.uint32
+I32 = mybir.dt.int32
+U8 = mybir.dt.uint8
+FP8X4 = mybir.dt.float8_e4m3fn_x4
+MULT = mybir.AluOpType.mult
+ADD = mybir.AluOpType.add
+SUB = mybir.AluOpType.subtract
+COPY = mybir.ActivationFunctionType.Copy
+
+P = 128
+PACK = 4
+GROUP = P * PACK
+GROUPS = 2
+FIELDS = 256
+WIDTH = 2 * FIELDS
+RE = slice(0, FIELDS)
+IM = slice(FIELDS, WIDTH)
+
+GS_IN = "p t m s -> p m t s"
+PACK_IN = "p t (c i) -> p c t i"
+PACK_OUT = "p (c i) t -> p c t i"
+G_IN = "p t (m s) -> p m t s"
+G_OUT = "p s m t -> p m t s"
+
+FLOPS = 2 * 4 * 2 * 256 * 1024 * 1024
+
+
+def tile_preconditionedbornseriestwoiterations_x1_kernel(tc, u0, v, g, c, out_0, out_1, out_2):
+    nc = tc.nc
+    with ExitStack() as ctx:
+        sb = ctx.enter_context(tc.tile_pool(name="sb", bufs=1))
+        ps = ctx.enter_context(tc.psum_pool(name="ps", bufs=1))
+        ctx.enter_context(tc.manual_schedule())
+
+        def tiles(name, shape, dtype, count):
+            return [sb.tile(shape, dtype, name="%s%d" % (name, i), align_bytes=64) for i in range(count)]
+
+        bank = [ps.tile([P, WIDTH], F32, name="bank%d" % i) for i in range(8)]
+        ident = sb.tile([P, P], F32, name="ident")
+        v_raw = sb.tile([P, 4, PACK], BF16, name="v_raw")
+        c_raw = sb.tile([P, 4, PACK], BF16, name="c_raw")
+        v32 = sb.tile([P, 2, 8], F32, name="v32")
+        c32 = sb.tile([P, 2, 8], F32, name="c32")
+        vi_neg, ci_neg, wr, wi, wi_neg, er, ei, ei_neg, s0, s1, s2, s3 = tiles("coef", [P, 8], F32, 12)
+        vr, vi, cr, ci = v32[:, 0, :], v32[:, 1, :], c32[:, 0, :], c32[:, 1, :]
+        u_rows = tiles("u_rows", [P, 4, GROUP], BF16, GROUPS)
+        u_words = tiles("u_words", [P, 2, WIDTH], F32, GROUPS)
+        g_rows = tiles("g_rows", [P, PACK, GROUP], BF16, 8)
+        g_packed = tiles("g_packed", [P, PACK, P, PACK], BF16, 8)
+        g_codes = tiles("g_codes", [P, GROUP], U32, 8)
+        g_scales = tiles("g_scales", [P, GROUP], U8, 8)
+        src = tiles("src", [P, PACK, WIDTH], F32, GROUPS)
+        cross = tiles("cross", [P, PACK, WIDTH], F32, GROUPS)
+        extra = tiles("extra", [P, PACK, WIDTH], F32, GROUPS)
+        y_round = u_rows
+        acc = tiles("acc", [P, PACK, WIDTH], F32, GROUPS)
+        src_packed = tiles("src_packed", [P, 3 * FIELDS, PACK], BF16, GROUPS)
+        src_codes = tiles("src_codes", [P, 3 * FIELDS], U32, 2 * GROUPS)
+        src_scales = tiles("src_scales", [P, 3 * FIELDS], U8, 2 * GROUPS)
+        y_packed = tiles("y_packed", [P, WIDTH, PACK], BF16, GROUPS)
+        y_codes = tiles("y_codes", [P, WIDTH], U32, GROUPS)
+        y_scales = tiles("y_scales", [P, WIDTH], U8, GROUPS)
+        y_rows = tiles("y_rows", [P, 4, GROUP], F32, GROUPS)
+
+        engines = {"S": nc.scalar, "V": nc.vector, "G": nc.gpsimd, "Y": nc.sync}
+
+        def chunk(part, k, j):
+            return 4 * j + 2 * k + part
+
+        def col(coef, grp, t):
+            return coef[:, PACK * grp + t : PACK * grp + t + 1]
+
+        def move(eng, out, in_):
+            if eng == "S":
+                nc.scalar.copy(out=out, in_=in_)
+            elif eng == "V":
+                nc.vector.tensor_copy(out=out, in_=in_)
+            else:
+                nc.gpsimd.tensor_scalar(out=out, in0=in_, scalar1=1.0, scalar2=0.0, op0=MULT, op1=ADD)
+
+        def load_u(grp):
+            rows = u0[:, :, GROUP * grp : GROUP * (grp + 1)].rearrange("c (h m) n -> m (c h) n", m=P)
+            nc.sync.dma_start(out=u_rows[grp][:], in_=rows)
+
+        def load_g(i):
+            part, k, j = i % 2, (i // 2) % 2, i // 4
+            rows = g[part, GROUP * k : GROUP * (k + 1), GROUP * j : GROUP * (j + 1)]
+            nc.sync.dma_start(out=g_rows[i][:], in_=rows.rearrange("(p t) n -> p t n", t=PACK))
+
+        def load_coef(raw, vec):
+            nc.scalar.dma_start(out=raw[:], in_=vec.rearrange("c (g p t) -> p (c g) t", p=P, t=PACK))
+
+        def widen(wide, neg, raw):
+            nc.vector.tensor_copy(out=wide[:].rearrange("p c x -> p (c x)"), in_=raw[:].rearrange("p x t -> p (x t)"))
+            nc.vector.tensor_scalar(out=neg[:], in0=wide[:, 1, :], scalar1=-1.0, scalar2=None, op0=MULT)
+
+        def products():
+            tt = nc.gpsimd.tensor_tensor
+            tt(out=s0[:], in0=vr, in1=cr, op=MULT)
+            tt(out=s1[:], in0=vi, in1=ci, op=MULT)
+            tt(out=s2[:], in0=vr, in1=ci, op=MULT)
+            tt(out=s3[:], in0=vi, in1=cr, op=MULT)
+            tt(out=wr[:], in0=s0[:], in1=s1[:], op=SUB)
+            tt(out=wi[:], in0=s2[:], in1=s3[:], op=ADD)
+            tt(out=s0[:], in0=cr, in1=cr, op=MULT)
+            tt(out=s1[:], in0=ci, in1=ci, op=MULT)
+            tt(out=s2[:], in0=cr, in1=ci, op=MULT)
+            nc.gpsimd.tensor_scalar(out=wi_neg[:], in0=wi[:], scalar1=-1.0, scalar2=0.0, op0=MULT, op1=ADD)
+            tt(out=s0[:], in0=s0[:], in1=s1[:], op=SUB)
+            tt(out=s2[:], in0=s2[:], in1=s2[:], op=ADD)
+            tt(out=er[:], in0=cr, in1=s0[:], op=SUB)
+            tt(out=ei[:], in0=ci, in1=s2[:], op=SUB)
+            tt(out=ei_neg[:], in0=s2[:], in1=ci, op=SUB)
+
+        def turn_u(grp):
+            for u in range(2):
+                for q in range(4):
+                    words = u_rows[grp][:, q, :].bitcast(F32)
+                    nc.tensor.transpose(bank[4 + 2 * grp + u][:, P * q : P * (q + 1)], words[:, u::2], ident[:])
+
+        def slot(words, t):
+            return words.bitcast(BF16).rearrange("p (x e) -> p e x", e=2)[:, t % 2, :]
+
+        def u_psum(grp, t):
+            return slot(bank[4 + 2 * grp + t // 2][:], t)
+
+        def scale_cross(out, x, k, k_neg):
+            nc.scalar.activation(out=out[:, RE], in_=x[:, IM], func=COPY, scale=k_neg)
+            nc.scalar.activation(out=out[:, IM], in_=x[:, RE], func=COPY, scale=k)
+
+        def add_direct(out, x, k, addend):
+            nc.vector.scalar_tensor_tensor(out=out, in0=x, scalar=k, in1=addend, op0=MULT, op1=ADD)
+
+        def add_cross(out, x, k, k_neg):
+            add_direct(out[:, RE], x[:, IM], k_neg, out[:, RE])
+            add_direct(out[:, IM], x[:, RE], k, out[:, IM])
+
+        def s0_cross(grp, t):
+            scale_cross(src[grp][:, t, :], u_psum(grp, t), col(vi, grp, t), col(vi_neg, grp, t))
+
+        def s0_direct(grp, t):
+            add_direct(src[grp][:, t, :], u_psum(grp, t), col(vr, grp, t), src[grp][:, t, :])
+
+        def keep_u(grp, u):
+            nc.scalar.copy(out=u_words[grp][:, u, :], in_=bank[4 + 2 * grp + u][:])
+
+        def order_in(x, lo, hi):
+            return x[:, :, lo:hi].rearrange(PACK_IN, i=4)
+
+        def order_out(x, lo, hi):
+            return x[:, lo:hi, :].rearrange(PACK_OUT, i=4)
+
+        def pack(eng, packed, x, lo, hi):
+            move(eng, order_out(packed, lo, hi), order_in(x, lo, hi))
+
+        def pack_src(eng, grp, lo, hi):
+            pack(eng, src_packed[grp][:, FIELDS:, :], src[grp], lo, hi)
+
+        def pack_sum(eng, grp, lo, hi):
+            engines[eng].tensor_tensor(out=order_out(src_packed[grp][:, FIELDS:, :], lo, hi), in0=order_in(src[grp], lo, hi), in1=order_in(cross[grp], lo, hi), op=ADD)
+
+        def negate(grp):
+            flat = src_packed[grp][:].rearrange("p x t -> p (x t)")
+            nc.vector.tensor_scalar(out=flat[:, : PACK * FIELDS], in0=flat[:, PACK * WIDTH :], scalar1=-1.0, scalar2=None, op0=MULT)
+
+        def quantize(codes, scales, packed, lo, hi):
+            flat = packed[:, lo:hi, :].rearrange("p x t -> p (x t)")
+            nc.vector.quantize_mx(out=codes[:, lo:hi].bitcast(FP8X4), scales=scales[:, lo:hi], in_=flat)
+
+        def quant_src(it, grp, lo, hi):
+            quantize(src_codes[2 * it + grp], src_scales[2 * it + grp], src_packed[grp], lo, hi)
+
+        def pack_g(eng, i, lo=0, hi=P):
+            move(eng, g_packed[i][:, :, lo:hi, :].rearrange(G_OUT), g_rows[i][:, :, PACK * lo : PACK * hi].rearrange(G_IN, s=PACK))
+
+        def pack_gs(eng, i, lo, hi):
+            move(eng, g_packed[i][:, lo:hi, :, :].rearrange(G_OUT), g_rows[i][:].rearrange("p t (m s) -> p t m s", s=PACK)[:, :, :, lo:hi].rearrange(GS_IN))
+
+        def quant_gs(i, lo, hi):
+            quantize(g_codes[i], g_scales[i], g_packed[i][:].rearrange("p s m t -> p (s m) t"), P * lo, P * hi)
+
+        def quant_g(i):
+            quantize(g_codes[i], g_scales[i], g_packed[i][:].rearrange("p s m t -> p (s m) t"), 0, GROUP)
+
+        def scatter(it, j, t, b, passes):
+            for k, part in passes:
+                i = chunk(part, k, j)
+                cols = slice(P * t, P * (t + 1))
+                window = slice(0, WIDTH) if part else slice(FIELDS, 3 * FIELDS)
+                nc.tensor.matmul_mx(
+                    out=bank[b][:],
+                    lhsT=g_codes[i][:, cols].bitcast(FP8X4),
+                    lhsT_scale=g_scales[i][:, cols],
+                    rhs=src_codes[2 * it + k][:, window].bitcast(FP8X4),
+                    rhs_scale=src_scales[2 * it + k][:, window],
+                    start=(k, part) == (0, 0),
+                    stop=(k, part) == (1, 1),
+                )
+
+        def h_scale(grp, t, b):
+            scale_cross(extra[grp][:, t, :], bank[b][:], col(ei, grp, t), col(ei_neg, grp, t))
+
+        def h_sum(grp, t):
+            nc.gpsimd.tensor_tensor(out=acc[grp][:, t, :], in0=acc[grp][:, t, :], in1=extra[grp][:, t, :], op=ADD)
+
+        def y_scale(grp, t, b):
+            scale_cross(cross[grp][:, t, :], bank[b][:], col(ci, grp, t), col(ci_neg, grp, t))
+
+        def y_sum(eng, grp, lo, hi):
+            engines[eng].tensor_tensor(out=order_out(y_packed[grp], lo, hi), in0=order_in(acc[grp], lo, hi), in1=order_in(cross[grp], lo, hi), op=ADD)
+
+        def turn_sum(grp, q, b):
+            for t in range(PACK):
+                for x, first in ((acc, True), (cross, False)):
+                    nc.tensor.matmul(bank[b][:, P * t : P * (t + 1)], lhsT=x[grp][:, t, P * q : P * (q + 1)], rhs=ident[:], start=first, stop=not first, is_transpose=True)
+
+        def y_half(grp, t, b, part):
+            if part:
+                add_direct(acc[grp][:, t, IM], bank[b][:, RE], col(ci, grp, t), acc[grp][:, t, IM])
+            else:
+                add_direct(acc[grp][:, t, RE], bank[b][:, IM], col(ci_neg, grp, t), acc[grp][:, t, RE])
+
+        def store_words(grp, lo, hi):
+            words = out_1[grp].rearrange("p m t -> p (m t)").bitcast(I32)
+            nc.sync.dma_start(out=words[:, lo:hi], in_=y_codes[grp][:, lo:hi].bitcast(I32))
+
+        def store_scales(eng, grp, quad):
+            rows = out_2[grp, 4 * quad : 4 * quad + 4, :].bitcast(I32)
+            engines[eng].dma_start(out=rows, in_=y_scales[grp][32 * quad : 32 * quad + 4, :].bitcast(I32))
+
+        def half(out, x, k, k_neg, part, addend):
+            dst, other, coef = (IM, RE, k) if part else (RE, IM, k_neg)
+            if addend:
+                add_direct(out[:, dst], x[:, other], coef, out[:, dst])
+            else:
+                nc.scalar.activation(out=out[:, dst], in_=x[:, other], func=COPY, scale=coef)
+
+        def a2_half(grp, t, part, onto):
+            half((src if onto else cross)[grp][:, t, :], bank[4 * grp + t][:], col(wi, grp, t), col(wi_neg, grp, t), part, onto)
+
+        def h_half(grp, t, part, onto):
+            half((acc if onto else extra)[grp][:, t, :], bank[4 * grp + t][:], col(ei, grp, t), col(ei_neg, grp, t), part, onto)
+
+        def y_part(grp, t, part, onto):
+            half((acc if onto else cross)[grp][:, t, :], bank[4 * grp + t][:], col(ci, grp, t), col(ci_neg, grp, t), part, onto)
+
+        def y_half_direct(grp, t, part, onto):
+            cols = IM if part else RE
+            x = bank[4 * grp + t][:, cols]
+            if onto:
+                add_direct(acc[grp][:, t, cols], x, col(cr, grp, t), acc[grp][:, t, cols])
+            else:
+                nc.scalar.activation(out=src[grp][:, t, cols], in_=x, func=COPY, scale=col(cr, grp, t))
+
+        def y_scale_direct(grp, t):
+            nc.scalar.activation(out=src[grp][:, t, :], in_=bank[4 * grp + t][:], func=COPY, scale=col(cr, grp, t))
+
+        def turn_terms(grp, q, b, terms):
+            for t in range(PACK):
+                for i, x in enumerate(terms):
+                    nc.tensor.matmul(bank[b][:, P * t : P * (t + 1)], lhsT=x[grp][:, t, P * q : P * (q + 1)], rhs=ident[:], start=i == 0, stop=i == len(terms) - 1, is_transpose=True)
+
+        def round_y(eng, grp, q, b):
+            move(eng, y_round[grp][:, q, :].rearrange("m (p t) -> m p t", t=PACK), bank[b][:].rearrange("m (t p) -> m p t", t=PACK))
+
+        def round_rows(eng, grp, q):
+            move(eng, y_round[grp][:, q, :], y_rows[grp][:, q, :])
+
+        def turn_back(grp, q, b):
+            words = y_round[grp][:, q, :].bitcast(F32)
+            for u in range(2):
+                nc.tensor.transpose(bank[b][:, P * u : P * (u + 1)], words[:, u::2], ident[:])
+
+        def words_y(eng, grp, q, b):
+            words = y_packed[grp][:, P * q : P * (q + 1), :].rearrange("p m t -> p (m t)").bitcast(F32)
+            move(eng, words.rearrange("p (m u) -> p m u", u=2), bank[b][:, : 2 * P].rearrange("p (u m) -> p m u", u=2))
+
+        def a2_direct(grp, t, b):
+            add_direct(src[grp][:, t, :], bank[b][:], col(wr, grp, t), src[grp][:, t, :])
+
+        def a2_cross(grp, t, b):
+            add_cross(src[grp][:, t, :], bank[b][:], col(wi, grp, t), col(wi_neg, grp, t))
+
+        def a2_scale(grp, t, b):
+            scale_cross(cross[grp][:, t, :], bank[b][:], col(wi, grp, t), col(wi_neg, grp, t))
+
+        def h_direct(grp, t, b):
+            add_direct(acc[grp][:, t, :], bank[b][:], col(er, grp, t), slot(u_words[grp][:, t // 2, :], t))
+
+        def h_cross(grp, t, b):
+            add_cross(acc[grp][:, t, :], bank[b][:], col(ei, grp, t), col(ei_neg, grp, t))
+
+        def y_direct(grp, t, b):
+            add_direct(acc[grp][:, t, :], bank[b][:], col(cr, grp, t), acc[grp][:, t, :])
+
+        def y_cross(grp, t, b):
+            add_cross(acc[grp][:, t, :], bank[b][:], col(ci, grp, t), col(ci_neg, grp, t))
+
+        def turn_y(grp, q, b):
+            for t in range(PACK):
+                nc.tensor.transpose(bank[b][:, P * t : P * (t + 1)], acc[grp][:, t, P * q : P * (q + 1)], ident[:])
+
+        def rows_y(eng, grp, q, b):
+            move(eng, y_rows[grp][:, q, :].rearrange("m (p t) -> m p t", t=PACK), bank[b][:].rearrange("m (t p) -> m p t", t=PACK))
+
+        def store_rows(grp, lo, hi):
+            rows = out_0[:, :, GROUP * grp : GROUP * (grp + 1)].rearrange("c (h m) n -> m (c h) n", m=P)
+            nc.sync.dma_start(out=rows[:, lo:hi, :], in_=y_rows[grp][:, lo:hi, :])
+
+        def store_planes(grp):
+            words = out_1[grp].rearrange("p m t -> p (m t)").bitcast(I32)
+            nc.sync.dma_start(out=words, in_=y_codes[grp][:].bitcast(I32))
+            for quad in range(4):
+                rows = out_2[grp, 4 * quad : 4 * quad + 4, :].bitcast(I32)
+                nc.sync.dma_start(out=rows, in_=y_scales[grp][32 * quad : 32 * quad + 4, :].bitcast(I32))
+
+        S, V, G, Y = "S", "V", "G", "Y"
+        K0, K1 = [(0, 0), (0, 1)], [(1, 0), (1, 1)]
+        T4 = range(PACK)
+        make_identity(nc, ident[:])
+        load_coef(v_raw, v)
+        widen(v32, vi_neg, v_raw)
+        load_u(0)
+        load_coef(c_raw, c)
+        load_g(0)
+        widen(c32, ci_neg, c_raw)
+        load_u(1)
+        turn_u(0)
+        s0_cross(0, 0)
+        s0_cross(0, 1)
+        s0_cross(0, 3)
+        s0_cross(0, 2)
+        turn_u(1)
+        pack_gs(V, 0, 2, 4)
+        load_g(4)
+        pack_gs(V, 0, 0, 2)
+        s0_cross(1, 0)
+        load_g(1)
+        s0_cross(1, 1)
+        s0_direct(0, 1)
+        s0_direct(0, 0)
+        pack_gs(V, 4, 0, 2)
+        products()
+        keep_u(1, 1)
+        s0_direct(0, 2)
+        s0_cross(1, 2)
+        s0_direct(1, 1)
+        load_g(5)
+        load_g(2)
+        s0_cross(1, 3)
+        s0_direct(0, 3)
+        s0_direct(1, 0)
+        keep_u(0, 1)
+        keep_u(1, 0)
+        s0_direct(1, 2)
+        s0_direct(1, 3)
+        pack_src(S, 0, 0, 256)
+        pack_src(V, 0, 256, 512)
+        quant_gs(0, 0, 2)
+        negate(0)
+        quant_gs(4, 0, 2)
+        pack_gs(G, 1, 0, 2)
+        load_g(3)
+        quant_src(0, 0, FIELDS, 3 * FIELDS)
+        load_g(7)
+        quant_gs(1, 0, 2)
+        scatter(0, 0, 1, 1, [(0, 0)])
+        scatter(0, 1, 1, 5, [(0, 0)])
+        pack_gs(S, 1, 2, 4)
+        pack_gs(G, 5, 0, 2)
+        quant_gs(0, 2, 4)
+        keep_u(0, 0)
+        pack_gs(S, 2, 0, 2)
+        scatter(0, 0, 0, 0, [(0, 0)])
+        scatter(0, 0, 3, 3, [(0, 0)])
+        pack_src(V, 1, 0, 256)
+        pack_gs(S, 3, 0, 2)
+        scatter(0, 0, 2, 2, [(0, 0)])
+        pack_src(V, 1, 256, 512)
+        scatter(0, 1, 0, 4, [(0, 0)])
+        quant_gs(1, 2, 4)
+        quant_src(0, 0, 0, FIELDS)
+        pack_gs(V, 2, 2, 4)
+        scatter(0, 0, 0, 0, [(0, 1)])
+        quant_gs(5, 0, 2)
+        quant_gs(2, 0, 2)
+        load_g(6)
+        pack_gs(S, 3, 2, 4)
+        quant_src(0, 1, FIELDS, 3 * FIELDS)
+        negate(1)
+        scatter(0, 0, 2, 2, [(0, 1)])
+        pack_gs(S, 5, 2, 4)
+        quant_gs(2, 2, 4)
+        quant_gs(3, 0, 2)
+        pack_gs(S, 6, 0, 2)
+        pack_gs(V, 4, 2, 4)
+        scatter(0, 0, 1, 1, [(0, 1)])
+        quant_src(0, 1, 0, FIELDS)
+        scatter(0, 0, 3, 3, [(0, 1)])
+        pack_gs(V, 7, 0, 2)
+        scatter(0, 1, 0, 4, [(0, 1)])
+        scatter(0, 0, 1, 1, [(1, 0)])
+        scatter(0, 0, 0, 0, [(1, 0)])
+        scatter(0, 0, 2, 2, [(1, 0)])
+        quant_gs(3, 2, 4)
+        quant_gs(4, 2, 4)
+        scatter(0, 1, 1, 5, [(0, 1)])
+        scatter(0, 0, 3, 3, [(1, 0)])
+        pack_gs(S, 6, 2, 4)
+        scatter(0, 0, 0, 0, [(1, 1)])
+        scatter(0, 0, 1, 1, [(1, 1)])
+        quant_gs(7, 0, 2)
+        quant_gs(6, 0, 2)
+        a2_half(0, 0, 1, False)
+        quant_gs(5, 2, 4)
+        scatter(0, 0, 3, 3, [(1, 1)])
+        scatter(0, 0, 2, 2, [(1, 1)])
+        a2_half(0, 3, 1, False)
+        h_half(0, 0, 0, False)
+        scatter(0, 1, 2, 6, [(0, 0)])
+        a2_direct(0, 1, 1)
+        pack_gs(S, 7, 2, 4)
+        scatter(0, 1, 3, 7, [(0, 0)])
+        a2_direct(0, 2, 2)
+        scatter(0, 1, 0, 4, [(1, 0)])
+        a2_half(0, 2, 1, False)
+        quant_gs(6, 2, 4)
+        a2_direct(0, 3, 3)
+        a2_half(0, 1, 1, False)
+        scatter(0, 1, 1, 5, [(1, 0)])
+        h_half(0, 2, 1, False)
+        scatter(0, 1, 2, 6, [(0, 1)])
+        a2_direct(0, 0, 0)
+        scatter(0, 1, 1, 5, [(1, 1)])
+        h_half(0, 2, 0, False)
+        scatter(0, 1, 3, 7, [(0, 1)])
+        h_half(0, 1, 1, False)
+        quant_gs(7, 2, 4)
+        scatter(0, 1, 3, 7, [(1, 0)])
+        scatter(0, 1, 0, 4, [(1, 1)])
+        a2_half(1, 1, 1, False)
+        scatter(0, 1, 2, 6, [(1, 0)])
+        scatter(0, 1, 2, 6, [(1, 1)])
+        a2_half(0, 0, 0, False)
+        pack_sum(G, 0, 384, 512)
+        h_half(0, 1, 0, False)
+        a2_half(1, 2, 1, False)
+        a2_direct(1, 0, 4)
+        pack_sum(G, 0, 256, 384)
+        scatter(0, 1, 3, 7, [(1, 1)])
+        h_direct(0, 3, 3)
+        a2_half(1, 0, 1, False)
+        a2_direct(1, 3, 7)
+        a2_half(1, 3, 1, False)
+        a2_direct(1, 1, 5)
+        a2_direct(1, 2, 6)
+        negate(0)
+        pack_sum(V, 1, 256, 384)
+        a2_half(0, 1, 0, False)
+        pack_sum(V, 1, 384, 512)
+        a2_half(0, 3, 0, False)
+        a2_half(0, 2, 0, False)
+        h_direct(1, 3, 7)
+        h_half(0, 3, 0, False)
+        pack_sum(G, 0, 128, 256)
+        h_half(0, 3, 1, False)
+        h_direct(0, 1, 1)
+        pack_sum(V, 0, 0, 128)
+        a2_half(1, 3, 0, False)
+        quant_src(1, 0, 0, FIELDS)
+        quant_src(1, 0, FIELDS, 3 * FIELDS)
+        h_direct(0, 2, 2)
+        scatter(1, 0, 1, 1, [(0, 0)])
+        h_half(1, 3, 0, True)
+        a2_half(1, 1, 0, False)
+        a2_half(1, 0, 0, False)
+        scatter(1, 0, 3, 3, [(0, 0)])
+        a2_half(1, 2, 0, False)
+        scatter(1, 0, 1, 1, [(0, 1)])
+        h_half(1, 3, 1, True)
+        scatter(1, 0, 2, 2, [(0, 0)])
+        negate(1)
+        scatter(1, 1, 3, 7, [(0, 0)])
+        h_direct(1, 2, 6)
+        scatter(1, 0, 2, 2, [(0, 1)])
+        h_direct(0, 0, 0)
+        scatter(1, 1, 3, 7, [(0, 1)])
+        h_half(0, 0, 1, False)
+        scatter(1, 0, 3, 3, [(0, 1)])
+        pack_sum(G, 1, 128, 256)
+        scatter(1, 0, 0, 0, [(0, 0)])
+        pack_sum(G, 1, 0, 128)
+        scatter(1, 0, 0, 0, [(0, 1)])
+        h_sum(0, 0)
+        quant_src(1, 1, 0, FIELDS)
+        h_sum(0, 3)
+        quant_src(1, 1, FIELDS, 3 * FIELDS)
+        scatter(1, 0, 1, 1, [(1, 0)])
+        scatter(1, 0, 0, 0, [(1, 0)])
+        scatter(1, 0, 0, 0, [(1, 1)])
+        h_direct(1, 1, 5)
+        scatter(1, 0, 1, 1, [(1, 1)])
+        scatter(1, 1, 3, 7, [(1, 0)])
+        h_sum(0, 2)
+        h_direct(1, 0, 4)
+        h_half(1, 2, 1, True)
+        scatter(1, 0, 3, 3, [(1, 0)])
+        scatter(1, 0, 3, 3, [(1, 1)])
+        h_half(1, 0, 1, True)
+        y_part(0, 0, 0, False)
+        y_part(0, 1, 1, False)
+        h_half(1, 2, 0, True)
+        scatter(1, 1, 2, 6, [(0, 0)])
+        scatter(1, 1, 3, 7, [(1, 1)])
+        h_half(1, 0, 0, True)
+        y_part(0, 0, 1, False)
+        h_half(1, 1, 0, True)
+        scatter(1, 0, 2, 2, [(1, 0)])
+        h_half(1, 1, 1, True)
+        scatter(1, 0, 2, 2, [(1, 1)])
+        y_direct(0, 3, 3)
+        scatter(1, 1, 1, 5, [(0, 0)])
+        scatter(1, 1, 0, 4, [(0, 0)])
+        y_direct(1, 3, 7)
+        h_sum(0, 1)
+        y_direct(0, 2, 2)
+        y_part(0, 3, 1, False)
+        scatter(1, 1, 0, 4, [(0, 1)])
+        scatter(1, 1, 2, 6, [(0, 1)])
+        y_part(0, 1, 0, False)
+        y_part(1, 3, 1, True)
+        scatter(1, 1, 0, 4, [(1, 0)])
+        y_direct(0, 0, 0)
+        y_part(0, 2, 1, False)
+        scatter(1, 1, 1, 5, [(0, 1)])
+        y_part(0, 2, 0, False)
+        y_part(0, 3, 0, False)
+        scatter(1, 1, 1, 5, [(1, 0)])
+        y_part(1, 3, 0, True)
+        y_direct(0, 1, 1)
+        scatter(1, 1, 2, 6, [(1, 0)])
+        scatter(1, 1, 0, 4, [(1, 1)])
+        scatter(1, 1, 1, 5, [(1, 1)])
+        scatter(1, 1, 2, 6, [(1, 1)])
+        y_direct(1, 0, 4)
+        y_direct(1, 2, 6)
+        turn_sum(0, 3, 3)
+        y_direct(1, 1, 5)
+        turn_sum(0, 2, 2)
+        y_part(1, 0, 1, True)
+        y_part(1, 1, 1, True)
+        rows_y(S, 0, 3, 3)
+        y_part(1, 0, 0, True)
+        turn_sum(0, 1, 1)
+        y_part(1, 1, 0, True)
+        store_rows(0, 3, 4)
+        rows_y(S, 0, 2, 2)
+        turn_sum(0, 0, 0)
+        y_part(1, 2, 1, True)
+        y_sum(G, 0, 256, 384)
+        rows_y(S, 0, 1, 1)
+        turn_y(1, 3, 3)
+        rows_y(S, 0, 0, 0)
+        store_rows(0, 2, 3)
+        turn_y(1, 2, 2)
+        store_rows(0, 1, 2)
+        y_part(1, 2, 0, True)
+        y_sum(G, 0, 384, 512)
+        quantize(y_codes[0], y_scales[0], y_packed[0], 256, 512)
+        pack(V, y_packed[1], acc[1], 256, 384)
+        y_sum(V, 0, 128, 256)
+        rows_y(S, 1, 3, 3)
+        pack(V, y_packed[1], acc[1], 128, 256)
+        y_sum(V, 0, 0, 128)
+        turn_y(1, 0, 0)
+        store_words(0, 256, 512)
+        store_rows(0, 0, 1)
+        pack(V, y_packed[1], acc[1], 384, 512)
+        rows_y(S, 1, 2, 2)
+        rows_y(S, 1, 0, 0)
+        store_rows(1, 3, 4)
+        pack(S, y_packed[1], acc[1], 0, 128)
+        store_rows(1, 2, 3)
+        quantize(y_codes[0], y_scales[0], y_packed[0], 0, 256)
+        store_rows(1, 0, 1)
+        store_words(0, 0, 256)
+        turn_y(1, 1, 1)
+        rows_y(S, 1, 1, 1)
+        quantize(y_codes[1], y_scales[1], y_packed[1], 256, 512)
+        store_scales(Y, 0, 3)
+        quantize(y_codes[1], y_scales[1], y_packed[1], 0, 256)
+        store_scales(Y, 0, 1)
+        store_scales(Y, 0, 2)
+        store_scales(S, 1, 3)
+        store_scales(S, 1, 2)
+        store_words(1, 0, 256)
+        store_scales(Y, 1, 0)
+        store_scales(Y, 1, 1)
+        store_rows(1, 1, 2)
+        store_words(1, 256, 512)
+        store_scales(Y, 0, 0)

@@ -89,10 +89,25 @@ def tile_preconditionedbornseriestwoiterations_x1_kernel(tc, u0, v, g, c, out_0,
             rows = u0[:, :, GROUP * grp : GROUP * (grp + 1)].rearrange("c (h m) n -> m (c h) n", m=P)
             nc.sync.dma_start(out=u_rows[grp][:], in_=rows)
 
+        def load_u_part(grp, lo, hi):
+            rows = u0[:, :, GROUP * grp : GROUP * (grp + 1)].rearrange("c (h m) n -> m (c h) n", m=P)
+            nc.sync.dma_start(out=u_rows[grp][:, lo:hi, :], in_=rows[:, lo:hi, :])
+
+        def turn_u_part(grp, lo, hi):
+            for q in range(lo, hi):
+                words = u_rows[grp][:, q, :].bitcast(F32)
+                for u in range(2):
+                    nc.tensor.transpose(bank[4 + 2 * grp + u][:, P * q : P * (q + 1)], words[:, u::2], ident[:])
+
         def load_g(i):
             part, k, j = i % 2, (i // 2) % 2, i // 4
             rows = g[part, GROUP * k : GROUP * (k + 1), GROUP * j : GROUP * (j + 1)]
             nc.sync.dma_start(out=g_rows[i][:], in_=rows.rearrange("(p t) n -> p t n", t=PACK))
+
+        def load_g_half(i, lo, hi):
+            part, k, j = i % 2, (i // 2) % 2, i // 4
+            rows = g[part, GROUP * k : GROUP * (k + 1), GROUP * j + PACK * lo : GROUP * j + PACK * hi]
+            nc.sync.dma_start(out=g_rows[i][:, :, PACK * lo : PACK * hi], in_=rows.rearrange("(p t) n -> p t n", t=PACK))
 
         def load_coef(raw, vec):
             nc.scalar.dma_start(out=raw[:], in_=vec.rearrange("c (g p t) -> p (c g) t", p=P, t=PACK))
@@ -145,6 +160,28 @@ def tile_preconditionedbornseriestwoiterations_x1_kernel(tc, u0, v, g, c, out_0,
         def s0_cross(grp, t):
             scale_cross(src[grp][:, t, :], u_psum(grp, t), col(vi, grp, t), col(vi_neg, grp, t))
 
+        def s0_half(eng, grp, t, part):
+            dst, other, coef = (IM, RE, vi) if part else (RE, IM, vi_neg)
+            out, x, k = src[grp][:, t, dst], u_psum(grp, t)[:, other], col(coef, grp, t)
+            if eng == "S":
+                nc.scalar.activation(out=out, in_=x, func=COPY, scale=k)
+            else:
+                nc.vector.tensor_scalar(out=out, in0=x, scalar1=k, scalar2=None, op0=MULT)
+
+        def a2_plain(grp, t):
+            nc.scalar.activation(out=cross[grp][:, t, :], in_=bank[4 * grp + t][:], func=COPY, scale=col(wi, grp, t))
+
+        def pack_mix(eng, grp, lo, hi):
+            other = (lo + FIELDS) % WIDTH
+            engines[eng].tensor_tensor(out=order_out(src_packed[grp][:, FIELDS:, :], lo, hi), in0=order_in(src[grp], lo, hi), in1=order_in(cross[grp], other, other + hi - lo), op=SUB if lo < FIELDS else ADD)
+
+        def h_plain(grp, t):
+            nc.scalar.activation(out=extra[grp][:, t, :], in_=bank[4 * grp + t][:], func=COPY, scale=col(ei, grp, t))
+
+        def h_mix(grp, lo, hi, part):
+            dst, other = (IM, RE) if part else (RE, IM)
+            nc.gpsimd.tensor_tensor(out=acc[grp][:, lo:hi, dst], in0=acc[grp][:, lo:hi, dst], in1=extra[grp][:, lo:hi, other], op=ADD if part else SUB)
+
         def s0_direct(grp, t):
             add_direct(src[grp][:, t, :], u_psum(grp, t), col(vr, grp, t), src[grp][:, t, :])
 
@@ -166,9 +203,18 @@ def tile_preconditionedbornseriestwoiterations_x1_kernel(tc, u0, v, g, c, out_0,
         def pack_sum(eng, grp, lo, hi):
             engines[eng].tensor_tensor(out=order_out(src_packed[grp][:, FIELDS:, :], lo, hi), in0=order_in(src[grp], lo, hi), in1=order_in(cross[grp], lo, hi), op=ADD)
 
-        def negate(grp):
+        def negate(eng, grp):
             flat = src_packed[grp][:].rearrange("p x t -> p (x t)")
-            nc.vector.tensor_scalar(out=flat[:, : PACK * FIELDS], in0=flat[:, PACK * WIDTH :], scalar1=-1.0, scalar2=None, op0=MULT)
+            out, x = flat[:, : PACK * FIELDS], flat[:, PACK * WIDTH :]
+            if eng == "V":
+                nc.vector.tensor_scalar(out=out, in0=x, scalar1=-1.0, scalar2=None, op0=MULT)
+            elif eng == "S":
+                nc.scalar.activation(out=out, in_=x, func=COPY, scale=-1.0)
+            else:
+                nc.gpsimd.tensor_scalar(out=out, in0=x, scalar1=-1.0, scalar2=0.0, op0=MULT, op1=ADD)
+
+        def merge(x, grp, t):
+            nc.gpsimd.tensor_tensor(out=x[grp][:, t, :], in0=x[grp][:, t, :], in1=cross[grp][:, t, :], op=ADD)
 
         def quantize(codes, scales, packed, lo, hi):
             flat = packed[:, lo:hi, :].rearrange("p x t -> p (x t)")
@@ -324,285 +370,270 @@ def tile_preconditionedbornseriestwoiterations_x1_kernel(tc, u0, v, g, c, out_0,
         S, V, G, Y = "S", "V", "G", "Y"
         K0, K1 = [(0, 0), (0, 1)], [(1, 0), (1, 1)]
         T4 = range(PACK)
-        make_identity(nc, ident[:])
         load_coef(v_raw, v)
-        widen(v32, vi_neg, v_raw)
-        load_u(0)
+        make_identity(nc, ident[:])
+        load_u_part(0, 0, 2)
+        load_u_part(0, 2, 4)
         load_coef(c_raw, c)
         load_g(0)
-        widen(c32, ci_neg, c_raw)
         load_u(1)
-        turn_u(0)
-        s0_cross(0, 0)
-        s0_cross(0, 1)
-        s0_cross(0, 3)
-        s0_cross(0, 2)
-        turn_u(1)
-        pack_gs(V, 0, 2, 4)
-        load_g(4)
-        pack_gs(V, 0, 0, 2)
-        s0_cross(1, 0)
         load_g(1)
-        s0_cross(1, 1)
-        s0_direct(0, 1)
-        s0_direct(0, 0)
-        pack_gs(V, 4, 0, 2)
-        products()
-        keep_u(1, 1)
-        s0_direct(0, 2)
-        s0_cross(1, 2)
-        s0_direct(1, 1)
-        load_g(5)
         load_g(2)
-        s0_cross(1, 3)
-        s0_direct(0, 3)
+        load_g(3)
+        load_g(4)
+        load_g(5)
+        load_g(6)
+        load_g(7)
+        widen(v32, vi_neg, v_raw)
+        turn_u_part(0, 0, 2)
+        widen(c32, ci_neg, c_raw)
+        products()
+        turn_u_part(0, 2, 4)
+        s0_half(S, 0, 0, 0)
+        pack_g(V, 0, 0, 128)
+        s0_half(S, 0, 0, 1)
+        s0_half(S, 0, 1, 0)
+        s0_half(S, 0, 1, 1)
+        turn_u(1)
+        s0_half(S, 0, 2, 0)
+        s0_direct(0, 0)
+        s0_half(S, 0, 2, 1)
+        s0_half(S, 0, 3, 0)
+        s0_direct(0, 1)
+        s0_half(S, 1, 0, 0)
+        s0_half(S, 1, 0, 1)
+        s0_direct(0, 2)
+        s0_half(S, 1, 1, 0)
+        s0_half(S, 1, 1, 1)
+        pack_g(V, 1, 0, 128)
+        s0_half(S, 0, 3, 1)
+        keep_u(0, 0)
+        s0_half(S, 1, 2, 0)
         s0_direct(1, 0)
-        keep_u(0, 1)
+        s0_half(S, 1, 2, 1)
+        s0_half(S, 1, 3, 0)
+        s0_direct(0, 3)
+        s0_half(S, 1, 3, 1)
+        s0_direct(1, 1)
+        pack_g(S, 2, 0, 128)
+        pack_src(V, 0, 0, 256)
+        pack_src(V, 0, 256, 512)
+        quant_g(0)
         keep_u(1, 0)
         s0_direct(1, 2)
-        s0_direct(1, 3)
-        pack_src(S, 0, 0, 256)
-        pack_src(V, 0, 256, 512)
-        quant_gs(0, 0, 2)
-        negate(0)
-        quant_gs(4, 0, 2)
-        pack_gs(G, 1, 0, 2)
-        load_g(3)
+        pack_g(S, 3, 0, 128)
         quant_src(0, 0, FIELDS, 3 * FIELDS)
-        load_g(7)
-        quant_gs(1, 0, 2)
-        scatter(0, 0, 1, 1, [(0, 0)])
-        scatter(0, 1, 1, 5, [(0, 0)])
-        pack_gs(S, 1, 2, 4)
-        pack_gs(G, 5, 0, 2)
-        quant_gs(0, 2, 4)
-        keep_u(0, 0)
-        pack_gs(S, 2, 0, 2)
+        negate(V, 0)
         scatter(0, 0, 0, 0, [(0, 0)])
-        scatter(0, 0, 3, 3, [(0, 0)])
-        pack_src(V, 1, 0, 256)
-        pack_gs(S, 3, 0, 2)
-        scatter(0, 0, 2, 2, [(0, 0)])
-        pack_src(V, 1, 256, 512)
-        scatter(0, 1, 0, 4, [(0, 0)])
-        quant_gs(1, 2, 4)
+        quant_g(1)
+        s0_direct(1, 3)
         quant_src(0, 0, 0, FIELDS)
-        pack_gs(V, 2, 2, 4)
+        pack_src(V, 1, 256, 512)
+        pack_src(S, 1, 0, 256)
         scatter(0, 0, 0, 0, [(0, 1)])
-        quant_gs(5, 0, 2)
-        quant_gs(2, 0, 2)
-        load_g(6)
-        pack_gs(S, 3, 2, 4)
-        quant_src(0, 1, FIELDS, 3 * FIELDS)
-        negate(1)
-        scatter(0, 0, 2, 2, [(0, 1)])
-        pack_gs(S, 5, 2, 4)
-        quant_gs(2, 2, 4)
-        quant_gs(3, 0, 2)
-        pack_gs(S, 6, 0, 2)
-        pack_gs(V, 4, 2, 4)
+        quant_g(2)
+        scatter(0, 0, 1, 1, [(0, 0)])
         scatter(0, 0, 1, 1, [(0, 1)])
+        negate(V, 1)
+        scatter(0, 0, 2, 2, [(0, 0)])
+        quant_src(0, 1, FIELDS, 3 * FIELDS)
+        scatter(0, 0, 2, 2, [(0, 1)])
         quant_src(0, 1, 0, FIELDS)
-        scatter(0, 0, 3, 3, [(0, 1)])
-        pack_gs(V, 7, 0, 2)
-        scatter(0, 1, 0, 4, [(0, 1)])
-        scatter(0, 0, 1, 1, [(1, 0)])
         scatter(0, 0, 0, 0, [(1, 0)])
-        scatter(0, 0, 2, 2, [(1, 0)])
-        quant_gs(3, 2, 4)
-        quant_gs(4, 2, 4)
-        scatter(0, 1, 1, 5, [(0, 1)])
-        scatter(0, 0, 3, 3, [(1, 0)])
-        pack_gs(S, 6, 2, 4)
+        pack_g(V, 4, 0, 128)
+        pack_g(S, 5, 0, 128)
+        scatter(0, 0, 3, 3, [(0, 0)])
+        pack_g(S, 6, 0, 128)
+        quant_g(3)
+        quant_g(4)
         scatter(0, 0, 0, 0, [(1, 1)])
+        scatter(0, 0, 1, 1, [(1, 0)])
+        quant_g(5)
         scatter(0, 0, 1, 1, [(1, 1)])
-        quant_gs(7, 0, 2)
-        quant_gs(6, 0, 2)
-        a2_half(0, 0, 1, False)
-        quant_gs(5, 2, 4)
-        scatter(0, 0, 3, 3, [(1, 1)])
-        scatter(0, 0, 2, 2, [(1, 1)])
-        a2_half(0, 3, 1, False)
-        h_half(0, 0, 0, False)
-        scatter(0, 1, 2, 6, [(0, 0)])
-        a2_direct(0, 1, 1)
-        pack_gs(S, 7, 2, 4)
-        scatter(0, 1, 3, 7, [(0, 0)])
-        a2_direct(0, 2, 2)
-        scatter(0, 1, 0, 4, [(1, 0)])
-        a2_half(0, 2, 1, False)
-        quant_gs(6, 2, 4)
-        a2_direct(0, 3, 3)
-        a2_half(0, 1, 1, False)
-        scatter(0, 1, 1, 5, [(1, 0)])
-        h_half(0, 2, 1, False)
-        scatter(0, 1, 2, 6, [(0, 1)])
+        scatter(0, 0, 3, 3, [(0, 1)])
         a2_direct(0, 0, 0)
-        scatter(0, 1, 1, 5, [(1, 1)])
-        h_half(0, 2, 0, False)
-        scatter(0, 1, 3, 7, [(0, 1)])
-        h_half(0, 1, 1, False)
-        quant_gs(7, 2, 4)
-        scatter(0, 1, 3, 7, [(1, 0)])
+        scatter(0, 0, 2, 2, [(1, 0)])
+        scatter(0, 1, 0, 4, [(0, 0)])
+        a2_direct(0, 1, 1)
+        pack_g(S, 7, 0, 64)
+        scatter(0, 0, 2, 2, [(1, 1)])
+        scatter(0, 0, 3, 3, [(1, 0)])
+        quant_g(6)
+        scatter(0, 1, 0, 4, [(0, 1)])
+        scatter(0, 0, 3, 3, [(1, 1)])
+        a2_half(0, 0, 0, True)
+        keep_u(0, 1)
+        scatter(0, 1, 0, 4, [(1, 0)])
+        a2_half(0, 0, 1, True)
+        a2_half(0, 1, 1, True)
+        pack_g(S, 7, 64, 128)
+        a2_direct(0, 2, 2)
+        scatter(0, 1, 1, 5, [(0, 0)])
+        scatter(0, 1, 1, 5, [(0, 1)])
+        a2_direct(0, 3, 3)
+        scatter(0, 1, 2, 6, [(0, 0)])
+        h_plain(0, 0)
+        a2_half(0, 2, 1, True)
+        quant_g(7)
+        h_plain(0, 1)
+        a2_half(0, 3, 1, True)
+        keep_u(1, 1)
         scatter(0, 1, 0, 4, [(1, 1)])
-        a2_half(1, 1, 1, False)
+        h_direct(0, 0, 0)
+        scatter(0, 1, 2, 6, [(0, 1)])
+        pack_src(S, 0, 256, 512)
+        scatter(0, 1, 1, 5, [(1, 0)])
+        a2_direct(1, 0, 4)
+        scatter(0, 1, 3, 7, [(0, 0)])
+        scatter(0, 1, 1, 5, [(1, 1)])
+        h_direct(0, 1, 1)
         scatter(0, 1, 2, 6, [(1, 0)])
         scatter(0, 1, 2, 6, [(1, 1)])
-        a2_half(0, 0, 0, False)
-        pack_sum(G, 0, 384, 512)
-        h_half(0, 1, 0, False)
-        a2_half(1, 2, 1, False)
-        a2_direct(1, 0, 4)
-        pack_sum(G, 0, 256, 384)
-        scatter(0, 1, 3, 7, [(1, 1)])
-        h_direct(0, 3, 3)
-        a2_half(1, 0, 1, False)
-        a2_direct(1, 3, 7)
-        a2_half(1, 3, 1, False)
+        a2_half(1, 0, 1, True)
+        h_plain(0, 2)
+        scatter(0, 1, 3, 7, [(0, 1)])
+        h_mix(0, 0, 2, 0)
+        a2_half(0, 1, 0, True)
+        scatter(0, 1, 3, 7, [(1, 0)])
+        negate(S, 0)
         a2_direct(1, 1, 5)
+        scatter(0, 1, 3, 7, [(1, 1)])
+        a2_half(0, 2, 0, True)
+        a2_half(0, 3, 0, True)
+        h_plain(1, 0)
+        a2_half(1, 1, 1, True)
+        h_mix(0, 0, 2, 1)
         a2_direct(1, 2, 6)
-        negate(0)
-        pack_sum(V, 1, 256, 384)
-        a2_half(0, 1, 0, False)
-        pack_sum(V, 1, 384, 512)
-        a2_half(0, 3, 0, False)
-        a2_half(0, 2, 0, False)
-        h_direct(1, 3, 7)
-        h_half(0, 3, 0, False)
-        pack_sum(G, 0, 128, 256)
-        h_half(0, 3, 1, False)
-        h_direct(0, 1, 1)
-        pack_sum(V, 0, 0, 128)
-        a2_half(1, 3, 0, False)
+        pack_src(S, 0, 0, 256)
+        a2_direct(1, 3, 7)
+        a2_half(1, 2, 1, True)
+        h_plain(1, 1)
+        a2_half(1, 3, 1, True)
         quant_src(1, 0, 0, FIELDS)
+        pack_src(S, 1, 256, 512)
         quant_src(1, 0, FIELDS, 3 * FIELDS)
-        h_direct(0, 2, 2)
-        scatter(1, 0, 1, 1, [(0, 0)])
-        h_half(1, 3, 0, True)
-        a2_half(1, 1, 0, False)
-        a2_half(1, 0, 0, False)
-        scatter(1, 0, 3, 3, [(0, 0)])
-        a2_half(1, 2, 0, False)
-        scatter(1, 0, 1, 1, [(0, 1)])
-        h_half(1, 3, 1, True)
-        scatter(1, 0, 2, 2, [(0, 0)])
-        negate(1)
-        scatter(1, 1, 3, 7, [(0, 0)])
-        h_direct(1, 2, 6)
-        scatter(1, 0, 2, 2, [(0, 1)])
-        h_direct(0, 0, 0)
-        scatter(1, 1, 3, 7, [(0, 1)])
-        h_half(0, 0, 1, False)
-        scatter(1, 0, 3, 3, [(0, 1)])
-        pack_sum(G, 1, 128, 256)
+        h_direct(1, 0, 4)
         scatter(1, 0, 0, 0, [(0, 0)])
-        pack_sum(G, 1, 0, 128)
+        a2_half(1, 0, 0, True)
+        h_plain(1, 2)
         scatter(1, 0, 0, 0, [(0, 1)])
-        h_sum(0, 0)
+        h_direct(1, 1, 5)
+        negate(S, 1)
+        scatter(1, 1, 0, 4, [(0, 0)])
+        a2_half(1, 1, 0, True)
+        h_mix(1, 0, 2, 0)
+        a2_half(1, 2, 0, True)
+        scatter(1, 0, 1, 1, [(0, 0)])
+        a2_half(1, 3, 0, True)
+        h_direct(0, 2, 2)
+        scatter(1, 0, 1, 1, [(0, 1)])
+        pack_src(S, 1, 0, 256)
+        scatter(1, 1, 0, 4, [(0, 1)])
+        scatter(1, 1, 1, 5, [(0, 0)])
+        h_direct(0, 3, 3)
+        scatter(1, 0, 2, 2, [(0, 0)])
+        scatter(1, 0, 2, 2, [(0, 1)])
         quant_src(1, 1, 0, FIELDS)
-        h_sum(0, 3)
+        scatter(1, 1, 1, 5, [(0, 1)])
+        h_plain(0, 3)
         quant_src(1, 1, FIELDS, 3 * FIELDS)
-        scatter(1, 0, 1, 1, [(1, 0)])
+        scatter(1, 0, 3, 3, [(0, 0)])
+        h_mix(0, 2, 4, 0)
+        h_direct(1, 2, 6)
         scatter(1, 0, 0, 0, [(1, 0)])
         scatter(1, 0, 0, 0, [(1, 1)])
-        h_direct(1, 1, 5)
+        h_direct(1, 3, 7)
+        scatter(1, 0, 1, 1, [(1, 0)])
         scatter(1, 0, 1, 1, [(1, 1)])
-        scatter(1, 1, 3, 7, [(1, 0)])
-        h_sum(0, 2)
-        h_direct(1, 0, 4)
-        h_half(1, 2, 1, True)
-        scatter(1, 0, 3, 3, [(1, 0)])
-        scatter(1, 0, 3, 3, [(1, 1)])
-        h_half(1, 0, 1, True)
-        y_part(0, 0, 0, False)
-        y_part(0, 1, 1, False)
-        h_half(1, 2, 0, True)
-        scatter(1, 1, 2, 6, [(0, 0)])
-        scatter(1, 1, 3, 7, [(1, 1)])
-        h_half(1, 0, 0, True)
-        y_part(0, 0, 1, False)
-        h_half(1, 1, 0, True)
-        scatter(1, 0, 2, 2, [(1, 0)])
-        h_half(1, 1, 1, True)
-        scatter(1, 0, 2, 2, [(1, 1)])
-        y_direct(0, 3, 3)
-        scatter(1, 1, 1, 5, [(0, 0)])
-        scatter(1, 1, 0, 4, [(0, 0)])
-        y_direct(1, 3, 7)
-        h_sum(0, 1)
-        y_direct(0, 2, 2)
-        y_part(0, 3, 1, False)
-        scatter(1, 1, 0, 4, [(0, 1)])
-        scatter(1, 1, 2, 6, [(0, 1)])
-        y_part(0, 1, 0, False)
-        y_part(1, 3, 1, True)
-        scatter(1, 1, 0, 4, [(1, 0)])
         y_direct(0, 0, 0)
-        y_part(0, 2, 1, False)
-        scatter(1, 1, 1, 5, [(0, 1)])
-        y_part(0, 2, 0, False)
-        y_part(0, 3, 0, False)
-        scatter(1, 1, 1, 5, [(1, 0)])
-        y_part(1, 3, 0, True)
+        scatter(1, 1, 2, 6, [(0, 0)])
+        h_plain(1, 3)
+        h_mix(0, 2, 4, 1)
+        scatter(1, 0, 2, 2, [(1, 0)])
         y_direct(0, 1, 1)
-        scatter(1, 1, 2, 6, [(1, 0)])
+        scatter(1, 0, 3, 3, [(0, 1)])
+        scatter(1, 1, 0, 4, [(1, 0)])
+        y_part(0, 0, 1, True)
+        scatter(1, 0, 2, 2, [(1, 1)])
+        y_part(0, 0, 0, True)
+        scatter(1, 0, 3, 3, [(1, 0)])
+        y_part(0, 1, 0, True)
+        scatter(1, 1, 2, 6, [(0, 1)])
+        h_mix(1, 0, 2, 1)
+        scatter(1, 0, 3, 3, [(1, 1)])
+        y_direct(0, 2, 2)
         scatter(1, 1, 0, 4, [(1, 1)])
+        scatter(1, 1, 1, 5, [(1, 0)])
+        y_direct(0, 3, 3)
+        scatter(1, 1, 3, 7, [(0, 0)])
         scatter(1, 1, 1, 5, [(1, 1)])
-        scatter(1, 1, 2, 6, [(1, 1)])
-        y_direct(1, 0, 4)
-        y_direct(1, 2, 6)
-        turn_sum(0, 3, 3)
-        y_direct(1, 1, 5)
-        turn_sum(0, 2, 2)
-        y_part(1, 0, 1, True)
-        y_part(1, 1, 1, True)
-        rows_y(S, 0, 3, 3)
-        y_part(1, 0, 0, True)
-        turn_sum(0, 1, 1)
-        y_part(1, 1, 0, True)
-        store_rows(0, 3, 4)
-        rows_y(S, 0, 2, 2)
-        turn_sum(0, 0, 0)
-        y_part(1, 2, 1, True)
-        y_sum(G, 0, 256, 384)
-        rows_y(S, 0, 1, 1)
-        turn_y(1, 3, 3)
+        h_mix(1, 2, 4, 0)
+        y_part(0, 2, 0, True)
+        scatter(1, 1, 2, 6, [(1, 0)])
+        y_part(0, 3, 0, True)
+        turn_y(0, 0, 0)
+        y_part(0, 1, 1, True)
+        y_part(0, 2, 1, True)
+        turn_y(0, 1, 1)
         rows_y(S, 0, 0, 0)
-        store_rows(0, 2, 3)
-        turn_y(1, 2, 2)
-        store_rows(0, 1, 2)
-        y_part(1, 2, 0, True)
-        y_sum(G, 0, 384, 512)
-        quantize(y_codes[0], y_scales[0], y_packed[0], 256, 512)
-        pack(V, y_packed[1], acc[1], 256, 384)
-        y_sum(V, 0, 128, 256)
-        rows_y(S, 1, 3, 3)
-        pack(V, y_packed[1], acc[1], 128, 256)
-        y_sum(V, 0, 0, 128)
-        turn_y(1, 0, 0)
-        store_words(0, 256, 512)
+        y_part(0, 3, 1, True)
+        turn_y(0, 2, 2)
+        y_direct(1, 0, 4)
+        h_mix(1, 2, 4, 1)
+        pack(S, y_packed[0], acc[0], 0, 256)
+        scatter(1, 1, 3, 7, [(0, 1)])
         store_rows(0, 0, 1)
-        pack(V, y_packed[1], acc[1], 384, 512)
-        rows_y(S, 1, 2, 2)
-        rows_y(S, 1, 0, 0)
-        store_rows(1, 3, 4)
-        pack(S, y_packed[1], acc[1], 0, 128)
-        store_rows(1, 2, 3)
+        y_direct(1, 1, 5)
+        turn_y(0, 3, 3)
+        y_part(1, 0, 0, True)
+        scatter(1, 1, 2, 6, [(1, 1)])
+        y_part(1, 1, 0, True)
+        rows_y(S, 0, 1, 1)
+        scatter(1, 1, 3, 7, [(1, 0)])
         quantize(y_codes[0], y_scales[0], y_packed[0], 0, 256)
-        store_rows(1, 0, 1)
+        scatter(1, 1, 3, 7, [(1, 1)])
+        pack(S, y_packed[0], acc[0], 256, 512)
+        y_direct(1, 2, 6)
         store_words(0, 0, 256)
+        store_rows(0, 1, 2)
+        y_direct(1, 3, 7)
+        y_part(1, 2, 0, True)
+        rows_y(S, 0, 2, 2)
+        y_part(1, 3, 0, True)
+        turn_y(1, 0, 0)
+        quantize(y_codes[0], y_scales[0], y_packed[0], 256, 512)
+        rows_y(S, 0, 3, 3)
+        store_rows(0, 2, 3)
+        y_part(1, 0, 1, True)
         turn_y(1, 1, 1)
-        rows_y(S, 1, 1, 1)
-        quantize(y_codes[1], y_scales[1], y_packed[1], 256, 512)
-        store_scales(Y, 0, 3)
-        quantize(y_codes[1], y_scales[1], y_packed[1], 0, 256)
+        store_scales(S, 0, 0)
         store_scales(Y, 0, 1)
+        y_part(1, 1, 1, True)
+        rows_y(S, 1, 0, 0)
+        store_rows(0, 3, 4)
+        store_words(0, 256, 512)
+        y_part(1, 2, 1, True)
         store_scales(Y, 0, 2)
-        store_scales(S, 1, 3)
-        store_scales(S, 1, 2)
-        store_words(1, 0, 256)
-        store_scales(Y, 1, 0)
-        store_scales(Y, 1, 1)
+        store_scales(Y, 0, 3)
+        rows_y(S, 1, 1, 1)
+        y_part(1, 3, 1, True)
+        turn_y(1, 2, 2)
+        store_rows(1, 0, 1)
+        pack(V, y_packed[1], acc[1], 0, 128)
+        pack(S, y_packed[1], acc[1], 128, 256)
+        turn_y(1, 3, 3)
         store_rows(1, 1, 2)
+        rows_y(V, 1, 2, 2)
+        pack(S, y_packed[1], acc[1], 256, 384)
+        quantize(y_codes[1], y_scales[1], y_packed[1], 0, 256)
+        store_rows(1, 2, 3)
+        pack(V, y_packed[1], acc[1], 384, 512)
+        rows_y(S, 1, 3, 3)
+        store_words(1, 0, 256)
+        quantize(y_codes[1], y_scales[1], y_packed[1], 256, 512)
+        store_rows(1, 3, 4)
+        store_scales(Y, 1, 0)
+        store_scales(S, 1, 1)
         store_words(1, 256, 512)
-        store_scales(Y, 0, 0)
+        store_scales(S, 1, 2)
+        store_scales(Y, 1, 3)

@@ -168,6 +168,11 @@ def tile_preconditionedbornseriestwoiterations_x1_kernel(tc, u0, v, g, c, out_0,
             else:
                 nc.vector.tensor_scalar(out=out, in0=x, scalar1=k, scalar2=None, op0=MULT)
 
+        def s0_pool(grp, t, part):
+            dst, other, coef = (IM, RE, vi) if part else (RE, IM, vi_neg)
+            x = slot(u_words[grp][:, t // 2, :], t)
+            nc.gpsimd.tensor_scalar(out=src[grp][:, t, dst], in0=x[:, other], scalar1=col(coef, grp, t), scalar2=0.0, op0=MULT, op1=ADD)
+
         def a2_plain(grp, t):
             nc.scalar.activation(out=cross[grp][:, t, :], in_=bank[4 * grp + t][:], func=COPY, scale=col(wi, grp, t))
 
@@ -371,8 +376,8 @@ def tile_preconditionedbornseriestwoiterations_x1_kernel(tc, u0, v, g, c, out_0,
         K0, K1 = [(0, 0), (0, 1)], [(1, 0), (1, 1)]
         T4 = range(PACK)
         load_coef(v_raw, v)
-        make_identity(nc, ident[:])
         load_u_part(0, 0, 2)
+        make_identity(nc, ident[:])
         load_u_part(0, 2, 4)
         load_coef(c_raw, c)
         load_g(0)
@@ -389,251 +394,260 @@ def tile_preconditionedbornseriestwoiterations_x1_kernel(tc, u0, v, g, c, out_0,
         widen(c32, ci_neg, c_raw)
         products()
         turn_u_part(0, 2, 4)
-        s0_half(S, 0, 0, 0)
-        pack_g(V, 0, 0, 128)
-        s0_half(S, 0, 0, 1)
+        s0_half(V, 0, 0, 0)
+        pack_g(S, 0, 0, 64)
+        s0_half(V, 0, 0, 1)
+        turn_u(1)
         s0_half(S, 0, 1, 0)
         s0_half(S, 0, 1, 1)
-        turn_u(1)
-        s0_half(S, 0, 2, 0)
-        s0_direct(0, 0)
-        s0_half(S, 0, 2, 1)
-        s0_half(S, 0, 3, 0)
-        s0_direct(0, 1)
+        s0_half(V, 0, 2, 0)
+        s0_half(V, 0, 2, 1)
+        s0_half(V, 0, 3, 0)
+        pack_g(V, 0, 64, 128)
         s0_half(S, 1, 0, 0)
+        pack_g(V, 1, 0, 64)
         s0_half(S, 1, 0, 1)
-        s0_direct(0, 2)
         s0_half(S, 1, 1, 0)
-        s0_half(S, 1, 1, 1)
-        pack_g(V, 1, 0, 128)
-        s0_half(S, 0, 3, 1)
-        keep_u(0, 0)
-        s0_half(S, 1, 2, 0)
-        s0_direct(1, 0)
-        s0_half(S, 1, 2, 1)
-        s0_half(S, 1, 3, 0)
-        s0_direct(0, 3)
-        s0_half(S, 1, 3, 1)
-        s0_direct(1, 1)
-        pack_g(S, 2, 0, 128)
-        pack_src(V, 0, 0, 256)
-        pack_src(V, 0, 256, 512)
         quant_g(0)
-        keep_u(1, 0)
+        s0_half(S, 1, 1, 1)
+        s0_half(S, 1, 2, 0)
+        pack_g(G, 1, 64, 128)
+        s0_half(V, 0, 3, 1)
+        pack_g(S, 2, 0, 64)
+        s0_direct(0, 0)
+        s0_half(V, 1, 2, 1)
+        s0_direct(0, 1)
+        s0_half(S, 1, 3, 0)
+        s0_direct(0, 2)
+        pack_g(S, 2, 64, 128)
+        pack_g(G, 3, 0, 64)
+        s0_direct(0, 3)
+        s0_direct(1, 0)
+        s0_half(S, 1, 3, 1)
+        pack_src(S, 0, 256, 512)
+        s0_direct(1, 1)
+        pack_src(G, 0, 0, 256)
         s0_direct(1, 2)
-        pack_g(S, 3, 0, 128)
-        quant_src(0, 0, FIELDS, 3 * FIELDS)
+        s0_direct(1, 3)
+        pack_g(S, 3, 64, 128)
         negate(V, 0)
+        pack_g(V, 4, 0, 64)
+        pack_src(S, 1, 0, 256)
+        quant_src(0, 0, FIELDS, 3 * FIELDS)
+        quant_src(0, 0, 0, FIELDS)
         scatter(0, 0, 0, 0, [(0, 0)])
         quant_g(1)
-        s0_direct(1, 3)
-        quant_src(0, 0, 0, FIELDS)
-        pack_src(V, 1, 256, 512)
-        pack_src(S, 1, 0, 256)
-        scatter(0, 0, 0, 0, [(0, 1)])
+        pack_g(S, 4, 64, 128)
         quant_g(2)
+        scatter(0, 0, 0, 0, [(0, 1)])
+        pack_src(V, 1, 256, 512)
+        pack_g(S, 5, 0, 64)
         scatter(0, 0, 1, 1, [(0, 0)])
+        quant_g(3)
         scatter(0, 0, 1, 1, [(0, 1)])
-        negate(V, 1)
         scatter(0, 0, 2, 2, [(0, 0)])
-        quant_src(0, 1, FIELDS, 3 * FIELDS)
+        negate(V, 1)
         scatter(0, 0, 2, 2, [(0, 1)])
+        quant_src(0, 1, FIELDS, 3 * FIELDS)
+        pack_g(S, 5, 64, 128)
+        scatter(0, 0, 3, 3, [(0, 0)])
         quant_src(0, 1, 0, FIELDS)
         scatter(0, 0, 0, 0, [(1, 0)])
-        pack_g(V, 4, 0, 128)
-        pack_g(S, 5, 0, 128)
-        scatter(0, 0, 3, 3, [(0, 0)])
-        pack_g(S, 6, 0, 128)
-        quant_g(3)
         quant_g(4)
         scatter(0, 0, 0, 0, [(1, 1)])
+        keep_u(0, 0)
         scatter(0, 0, 1, 1, [(1, 0)])
         quant_g(5)
-        scatter(0, 0, 1, 1, [(1, 1)])
         scatter(0, 0, 3, 3, [(0, 1)])
+        pack_g(S, 6, 0, 64)
+        scatter(0, 0, 1, 1, [(1, 1)])
         a2_direct(0, 0, 0)
-        scatter(0, 0, 2, 2, [(1, 0)])
         scatter(0, 1, 0, 4, [(0, 0)])
+        scatter(0, 0, 2, 2, [(1, 0)])
         a2_direct(0, 1, 1)
-        pack_g(S, 7, 0, 64)
         scatter(0, 0, 2, 2, [(1, 1)])
         scatter(0, 0, 3, 3, [(1, 0)])
-        quant_g(6)
-        scatter(0, 1, 0, 4, [(0, 1)])
-        scatter(0, 0, 3, 3, [(1, 1)])
-        a2_half(0, 0, 0, True)
         keep_u(0, 1)
-        scatter(0, 1, 0, 4, [(1, 0)])
         a2_half(0, 0, 1, True)
-        a2_half(0, 1, 1, True)
-        pack_g(S, 7, 64, 128)
+        scatter(0, 0, 3, 3, [(1, 1)])
+        pack_g(G, 6, 64, 128)
+        scatter(0, 1, 0, 4, [(0, 1)])
         a2_direct(0, 2, 2)
+        pack_g(S, 7, 0, 64)
         scatter(0, 1, 1, 5, [(0, 0)])
-        scatter(0, 1, 1, 5, [(0, 1)])
         a2_direct(0, 3, 3)
+        scatter(0, 1, 1, 5, [(0, 1)])
+        h_direct(0, 0, 0)
+        keep_u(1, 0)
+        quant_g(6)
+        pack_g(S, 7, 64, 128)
         scatter(0, 1, 2, 6, [(0, 0)])
-        h_plain(0, 0)
+        a2_half(0, 1, 1, True)
+        scatter(0, 1, 0, 4, [(1, 0)])
         a2_half(0, 2, 1, True)
-        quant_g(7)
-        h_plain(0, 1)
+        scatter(0, 1, 2, 6, [(0, 1)])
         a2_half(0, 3, 1, True)
         keep_u(1, 1)
-        scatter(0, 1, 0, 4, [(1, 1)])
-        h_direct(0, 0, 0)
-        scatter(0, 1, 2, 6, [(0, 1)])
-        pack_src(S, 0, 256, 512)
-        scatter(0, 1, 1, 5, [(1, 0)])
-        a2_direct(1, 0, 4)
-        scatter(0, 1, 3, 7, [(0, 0)])
-        scatter(0, 1, 1, 5, [(1, 1)])
+        quant_g(7)
+        h_plain(0, 0)
+        pack_src(G, 0, 256, 512)
         h_direct(0, 1, 1)
+        scatter(0, 1, 0, 4, [(1, 1)])
+        scatter(0, 1, 1, 5, [(1, 0)])
+        a2_half(0, 0, 0, True)
+        scatter(0, 1, 1, 5, [(1, 1)])
+        h_plain(0, 1)
+        a2_direct(1, 0, 4)
         scatter(0, 1, 2, 6, [(1, 0)])
-        scatter(0, 1, 2, 6, [(1, 1)])
-        a2_half(1, 0, 1, True)
+        scatter(0, 1, 3, 7, [(0, 0)])
         h_plain(0, 2)
+        a2_direct(1, 1, 5)
         scatter(0, 1, 3, 7, [(0, 1)])
         h_mix(0, 0, 2, 0)
-        a2_half(0, 1, 0, True)
-        scatter(0, 1, 3, 7, [(1, 0)])
+        scatter(0, 1, 2, 6, [(1, 1)])
         negate(S, 0)
-        a2_direct(1, 1, 5)
+        a2_half(1, 0, 1, True)
+        scatter(0, 1, 3, 7, [(1, 0)])
+        a2_half(0, 1, 0, True)
         scatter(0, 1, 3, 7, [(1, 1)])
         a2_half(0, 2, 0, True)
         a2_half(0, 3, 0, True)
-        h_plain(1, 0)
-        a2_half(1, 1, 1, True)
-        h_mix(0, 0, 2, 1)
         a2_direct(1, 2, 6)
+        h_mix(0, 0, 2, 1)
         pack_src(S, 0, 0, 256)
         a2_direct(1, 3, 7)
+        a2_half(1, 1, 1, True)
         a2_half(1, 2, 1, True)
-        h_plain(1, 1)
+        h_plain(1, 0)
         a2_half(1, 3, 1, True)
-        quant_src(1, 0, 0, FIELDS)
-        pack_src(S, 1, 256, 512)
         quant_src(1, 0, FIELDS, 3 * FIELDS)
+        h_plain(1, 1)
         h_direct(1, 0, 4)
+        pack_src(S, 1, 256, 512)
         scatter(1, 0, 0, 0, [(0, 0)])
-        a2_half(1, 0, 0, True)
-        h_plain(1, 2)
-        scatter(1, 0, 0, 0, [(0, 1)])
         h_direct(1, 1, 5)
-        negate(S, 1)
-        scatter(1, 1, 0, 4, [(0, 0)])
-        a2_half(1, 1, 0, True)
+        quant_src(1, 0, 0, FIELDS)
+        h_plain(1, 2)
         h_mix(1, 0, 2, 0)
+        a2_half(1, 0, 0, True)
+        scatter(1, 0, 0, 0, [(0, 1)])
+        a2_half(1, 1, 0, True)
+        negate(S, 1)
         a2_half(1, 2, 0, True)
         scatter(1, 0, 1, 1, [(0, 0)])
         a2_half(1, 3, 0, True)
         h_direct(0, 2, 2)
         scatter(1, 0, 1, 1, [(0, 1)])
         pack_src(S, 1, 0, 256)
+        scatter(1, 1, 0, 4, [(0, 0)])
+        h_mix(1, 0, 2, 1)
+        h_direct(1, 2, 6)
         scatter(1, 1, 0, 4, [(0, 1)])
         scatter(1, 1, 1, 5, [(0, 0)])
+        scatter(1, 1, 1, 5, [(0, 1)])
         h_direct(0, 3, 3)
+        scatter(1, 1, 2, 6, [(0, 0)])
+        scatter(1, 1, 2, 6, [(0, 1)])
+        quant_src(1, 1, FIELDS, 3 * FIELDS)
         scatter(1, 0, 2, 2, [(0, 0)])
+        h_plain(0, 3)
         scatter(1, 0, 2, 2, [(0, 1)])
         quant_src(1, 1, 0, FIELDS)
-        scatter(1, 1, 1, 5, [(0, 1)])
-        h_plain(0, 3)
-        quant_src(1, 1, FIELDS, 3 * FIELDS)
-        scatter(1, 0, 3, 3, [(0, 0)])
-        h_mix(0, 2, 4, 0)
-        h_direct(1, 2, 6)
         scatter(1, 0, 0, 0, [(1, 0)])
-        scatter(1, 0, 0, 0, [(1, 1)])
         h_direct(1, 3, 7)
+        h_mix(0, 2, 4, 0)
+        scatter(1, 1, 0, 4, [(1, 0)])
+        scatter(1, 1, 0, 4, [(1, 1)])
+        scatter(1, 0, 0, 0, [(1, 1)])
+        h_plain(1, 3)
+        y_direct(1, 0, 4)
         scatter(1, 0, 1, 1, [(1, 0)])
         scatter(1, 0, 1, 1, [(1, 1)])
-        y_direct(0, 0, 0)
-        scatter(1, 1, 2, 6, [(0, 0)])
-        h_plain(1, 3)
+        y_part(0, 0, 0, False)
+        scatter(1, 0, 3, 3, [(0, 0)])
         h_mix(0, 2, 4, 1)
+        y_part(1, 0, 0, True)
         scatter(1, 0, 2, 2, [(1, 0)])
+        scatter(1, 1, 1, 5, [(1, 0)])
+        y_direct(0, 0, 0)
+        scatter(1, 1, 1, 5, [(1, 1)])
+        scatter(1, 0, 2, 2, [(1, 1)])
         y_direct(0, 1, 1)
         scatter(1, 0, 3, 3, [(0, 1)])
-        scatter(1, 1, 0, 4, [(1, 0)])
-        y_part(0, 0, 1, True)
-        scatter(1, 0, 2, 2, [(1, 1)])
-        y_part(0, 0, 0, True)
+        y_part(0, 0, 1, False)
         scatter(1, 0, 3, 3, [(1, 0)])
-        y_part(0, 1, 0, True)
-        scatter(1, 1, 2, 6, [(0, 1)])
-        h_mix(1, 0, 2, 1)
+        h_mix(1, 2, 4, 0)
         scatter(1, 0, 3, 3, [(1, 1)])
         y_direct(0, 2, 2)
-        scatter(1, 1, 0, 4, [(1, 1)])
-        scatter(1, 1, 1, 5, [(1, 0)])
-        y_direct(0, 3, 3)
+        y_part(0, 1, 1, False)
         scatter(1, 1, 3, 7, [(0, 0)])
-        scatter(1, 1, 1, 5, [(1, 1)])
-        h_mix(1, 2, 4, 0)
-        y_part(0, 2, 0, True)
+        y_part(0, 1, 0, False)
         scatter(1, 1, 2, 6, [(1, 0)])
-        y_part(0, 3, 0, True)
-        turn_y(0, 0, 0)
-        y_part(0, 1, 1, True)
-        y_part(0, 2, 1, True)
-        turn_y(0, 1, 1)
-        rows_y(S, 0, 0, 0)
-        y_part(0, 3, 1, True)
-        turn_y(0, 2, 2)
-        y_direct(1, 0, 4)
-        h_mix(1, 2, 4, 1)
-        pack(S, y_packed[0], acc[0], 0, 256)
-        scatter(1, 1, 3, 7, [(0, 1)])
-        store_rows(0, 0, 1)
-        y_direct(1, 1, 5)
-        turn_y(0, 3, 3)
-        y_part(1, 0, 0, True)
+        y_direct(0, 3, 3)
         scatter(1, 1, 2, 6, [(1, 1)])
+        y_part(0, 2, 0, False)
+        scatter(1, 1, 3, 7, [(0, 1)])
+        y_part(1, 0, 1, True)
+        h_mix(1, 2, 4, 1)
+        y_part(0, 3, 0, False)
+        turn_sum(0, 0, 0)
+        y_direct(1, 1, 5)
+        y_part(0, 2, 1, False)
+        y_part(0, 3, 1, False)
+        turn_sum(0, 1, 1)
+        y_part(1, 1, 1, True)
+        rows_y(S, 0, 0, 0)
         y_part(1, 1, 0, True)
-        rows_y(S, 0, 1, 1)
         scatter(1, 1, 3, 7, [(1, 0)])
-        quantize(y_codes[0], y_scales[0], y_packed[0], 0, 256)
+        y_sum(G, 0, 0, 128)
+        rows_y(S, 0, 1, 1)
         scatter(1, 1, 3, 7, [(1, 1)])
-        pack(S, y_packed[0], acc[0], 256, 512)
         y_direct(1, 2, 6)
-        store_words(0, 0, 256)
-        store_rows(0, 1, 2)
+        store_rows(0, 0, 1)
+        turn_sum(0, 2, 2)
         y_direct(1, 3, 7)
+        store_rows(0, 1, 2)
+        turn_sum(0, 3, 3)
         y_part(1, 2, 0, True)
+        y_sum(G, 0, 128, 256)
         rows_y(S, 0, 2, 2)
         y_part(1, 3, 0, True)
         turn_y(1, 0, 0)
-        quantize(y_codes[0], y_scales[0], y_packed[0], 256, 512)
+        y_part(1, 2, 1, True)
         rows_y(S, 0, 3, 3)
         store_rows(0, 2, 3)
-        y_part(1, 0, 1, True)
-        turn_y(1, 1, 1)
-        store_scales(S, 0, 0)
-        store_scales(Y, 0, 1)
-        y_part(1, 1, 1, True)
-        rows_y(S, 1, 0, 0)
-        store_rows(0, 3, 4)
-        store_words(0, 256, 512)
-        y_part(1, 2, 1, True)
-        store_scales(Y, 0, 2)
-        store_scales(Y, 0, 3)
-        rows_y(S, 1, 1, 1)
         y_part(1, 3, 1, True)
+        turn_y(1, 1, 1)
+        rows_y(V, 1, 0, 0)
         turn_y(1, 2, 2)
-        store_rows(1, 0, 1)
-        pack(V, y_packed[1], acc[1], 0, 128)
-        pack(S, y_packed[1], acc[1], 128, 256)
+        store_rows(0, 3, 4)
+        rows_y(S, 1, 1, 1)
         turn_y(1, 3, 3)
+        y_sum(V, 0, 256, 384)
+        store_rows(1, 0, 1)
+        rows_y(S, 1, 2, 2)
         store_rows(1, 1, 2)
-        rows_y(V, 1, 2, 2)
-        pack(S, y_packed[1], acc[1], 256, 384)
-        quantize(y_codes[1], y_scales[1], y_packed[1], 0, 256)
-        store_rows(1, 2, 3)
-        pack(V, y_packed[1], acc[1], 384, 512)
+        pack(V, y_packed[1], acc[1], 0, 128)
         rows_y(S, 1, 3, 3)
-        store_words(1, 0, 256)
-        quantize(y_codes[1], y_scales[1], y_packed[1], 256, 512)
+        y_sum(V, 0, 384, 512)
+        store_rows(1, 2, 3)
+        pack(S, y_packed[1], acc[1], 128, 256)
+        quantize(y_codes[0], y_scales[0], y_packed[0], 0, 256)
         store_rows(1, 3, 4)
+        quantize(y_codes[0], y_scales[0], y_packed[0], 256, 512)
+        store_words(0, 0, 256)
+        pack(V, y_packed[1], acc[1], 256, 384)
+        pack(S, y_packed[1], acc[1], 384, 512)
+        store_words(0, 256, 512)
+        quantize(y_codes[1], y_scales[1], y_packed[1], 0, 256)
+        store_scales(S, 0, 0)
+        store_scales(S, 0, 1)
+        store_scales(S, 0, 2)
+        store_scales(S, 0, 3)
+        quantize(y_codes[1], y_scales[1], y_packed[1], 256, 512)
+        store_words(1, 0, 256)
         store_scales(Y, 1, 0)
         store_scales(S, 1, 1)
+        store_scales(Y, 1, 2)
+        store_scales(S, 1, 3)
         store_words(1, 256, 512)
-        store_scales(S, 1, 2)
-        store_scales(Y, 1, 3)

from contextlib import ExitStack

import concourse.mybir as mybir
from concourse.masks import make_identity

F32 = mybir.dt.float32
BF16 = mybir.dt.bfloat16
U32 = mybir.dt.uint32
I32 = mybir.dt.int32
U8 = mybir.dt.uint8
FP8X4 = mybir.dt.float8_e4m3fn_x4
MULT = mybir.AluOpType.mult
ADD = mybir.AluOpType.add
SUB = mybir.AluOpType.subtract
COPY = mybir.ActivationFunctionType.Copy

P = 128
PACK = 4
GROUP = P * PACK
GROUPS = 2
FIELDS = 256
WIDTH = 2 * FIELDS
RE = slice(0, FIELDS)
IM = slice(FIELDS, WIDTH)

GS_IN = "p t m s -> p m t s"
PACK_IN = "p t (c i) -> p c t i"
PACK_OUT = "p (c i) t -> p c t i"
G_IN = "p t (m s) -> p m t s"
G_OUT = "p s m t -> p m t s"

FLOPS = 2 * 4 * 2 * 256 * 1024 * 1024


def tile_preconditionedbornseriestwoiterations_x1_kernel(tc, u0, v, g, c, out_0, out_1, out_2):
    nc = tc.nc
    with ExitStack() as ctx:
        sb = ctx.enter_context(tc.tile_pool(name="sb", bufs=1))
        ps = ctx.enter_context(tc.psum_pool(name="ps", bufs=1))
        ctx.enter_context(tc.manual_schedule())

        def tiles(name, shape, dtype, count):
            return [sb.tile(shape, dtype, name="%s%d" % (name, i), align_bytes=64) for i in range(count)]

        bank = [ps.tile([P, WIDTH], F32, name="bank%d" % i) for i in range(8)]
        ident = sb.tile([P, P], F32, name="ident")
        v_raw = sb.tile([P, 4, PACK], BF16, name="v_raw")
        c_raw = sb.tile([P, 4, PACK], BF16, name="c_raw")
        v32 = sb.tile([P, 2, 8], F32, name="v32")
        c32 = sb.tile([P, 2, 8], F32, name="c32")
        vi_neg, ci_neg, wr, wi, wi_neg, er, ei, ei_neg, s0, s1, s2, s3 = tiles("coef", [P, 8], F32, 12)
        vr, vi, cr, ci = v32[:, 0, :], v32[:, 1, :], c32[:, 0, :], c32[:, 1, :]
        u_rows = tiles("u_rows", [P, 4, GROUP], BF16, GROUPS)
        u_words = tiles("u_words", [P, 2, WIDTH], F32, GROUPS)
        g_rows = tiles("g_rows", [P, PACK, GROUP], BF16, 8)
        g_packed = tiles("g_packed", [P, PACK, P, PACK], BF16, 8)
        g_codes = tiles("g_codes", [P, GROUP], U32, 8)
        g_scales = tiles("g_scales", [P, GROUP], U8, 8)
        src = tiles("src", [P, PACK, WIDTH], F32, GROUPS)
        cross = tiles("cross", [P, PACK, WIDTH], F32, GROUPS)
        extra = tiles("extra", [P, PACK, WIDTH], F32, GROUPS)
        y_round = u_rows
        acc = tiles("acc", [P, PACK, WIDTH], F32, GROUPS)
        src_packed = tiles("src_packed", [P, 3 * FIELDS, PACK], BF16, GROUPS)
        src_codes = tiles("src_codes", [P, 3 * FIELDS], U32, 2 * GROUPS)
        src_scales = tiles("src_scales", [P, 3 * FIELDS], U8, 2 * GROUPS)
        y_packed = tiles("y_packed", [P, WIDTH, PACK], BF16, GROUPS)
        y_codes = tiles("y_codes", [P, WIDTH], U32, GROUPS)
        y_scales = tiles("y_scales", [P, WIDTH], U8, GROUPS)
        y_rows = tiles("y_rows", [P, 4, GROUP], F32, GROUPS)

        engines = {"S": nc.scalar, "V": nc.vector, "G": nc.gpsimd, "Y": nc.sync}

        def chunk(part, k, j):
            return 4 * j + 2 * k + part

        def col(coef, grp, t):
            return coef[:, PACK * grp + t : PACK * grp + t + 1]

        def move(eng, out, in_):
            if eng == "S":
                nc.scalar.copy(out=out, in_=in_)
            elif eng == "V":
                nc.vector.tensor_copy(out=out, in_=in_)
            else:
                nc.gpsimd.tensor_scalar(out=out, in0=in_, scalar1=1.0, scalar2=0.0, op0=MULT, op1=ADD)

        def load_u(grp):
            rows = u0[:, :, GROUP * grp : GROUP * (grp + 1)].rearrange("c (h m) n -> m (c h) n", m=P)
            nc.sync.dma_start(out=u_rows[grp][:], in_=rows)

        def load_u_part(grp, lo, hi):
            rows = u0[:, :, GROUP * grp : GROUP * (grp + 1)].rearrange("c (h m) n -> m (c h) n", m=P)
            nc.sync.dma_start(out=u_rows[grp][:, lo:hi, :], in_=rows[:, lo:hi, :])

        def turn_u_part(grp, lo, hi):
            for q in range(lo, hi):
                words = u_rows[grp][:, q, :].bitcast(F32)
                for u in range(2):
                    nc.tensor.transpose(bank[4 + 2 * grp + u][:, P * q : P * (q + 1)], words[:, u::2], ident[:])

        def load_g(i):
            part, k, j = i % 2, (i // 2) % 2, i // 4
            rows = g[part, GROUP * k : GROUP * (k + 1), GROUP * j : GROUP * (j + 1)]
            nc.sync.dma_start(out=g_rows[i][:], in_=rows.rearrange("(p t) n -> p t n", t=PACK))

        def load_g_half(i, lo, hi):
            part, k, j = i % 2, (i // 2) % 2, i // 4
            rows = g[part, GROUP * k : GROUP * (k + 1), GROUP * j + PACK * lo : GROUP * j + PACK * hi]
            nc.sync.dma_start(out=g_rows[i][:, :, PACK * lo : PACK * hi], in_=rows.rearrange("(p t) n -> p t n", t=PACK))

        def load_coef(raw, vec):
            nc.scalar.dma_start(out=raw[:], in_=vec.rearrange("c (g p t) -> p (c g) t", p=P, t=PACK))

        def widen(wide, neg, raw):
            nc.vector.tensor_copy(out=wide[:].rearrange("p c x -> p (c x)"), in_=raw[:].rearrange("p x t -> p (x t)"))
            nc.vector.tensor_scalar(out=neg[:], in0=wide[:, 1, :], scalar1=-1.0, scalar2=None, op0=MULT)

        def products():
            tt = nc.gpsimd.tensor_tensor
            tt(out=s0[:], in0=vr, in1=cr, op=MULT)
            tt(out=s1[:], in0=vi, in1=ci, op=MULT)
            tt(out=s2[:], in0=vr, in1=ci, op=MULT)
            tt(out=s3[:], in0=vi, in1=cr, op=MULT)
            tt(out=wr[:], in0=s0[:], in1=s1[:], op=SUB)
            tt(out=wi[:], in0=s2[:], in1=s3[:], op=ADD)
            tt(out=s0[:], in0=cr, in1=cr, op=MULT)
            tt(out=s1[:], in0=ci, in1=ci, op=MULT)
            tt(out=s2[:], in0=cr, in1=ci, op=MULT)
            nc.gpsimd.tensor_scalar(out=wi_neg[:], in0=wi[:], scalar1=-1.0, scalar2=0.0, op0=MULT, op1=ADD)
            tt(out=s0[:], in0=s0[:], in1=s1[:], op=SUB)
            tt(out=s2[:], in0=s2[:], in1=s2[:], op=ADD)
            tt(out=er[:], in0=cr, in1=s0[:], op=SUB)
            tt(out=ei[:], in0=ci, in1=s2[:], op=SUB)
            tt(out=ei_neg[:], in0=s2[:], in1=ci, op=SUB)

        def turn_u(grp):
            for u in range(2):
                for q in range(4):
                    words = u_rows[grp][:, q, :].bitcast(F32)
                    nc.tensor.transpose(bank[4 + 2 * grp + u][:, P * q : P * (q + 1)], words[:, u::2], ident[:])

        def slot(words, t):
            return words.bitcast(BF16).rearrange("p (x e) -> p e x", e=2)[:, t % 2, :]

        def u_psum(grp, t):
            return slot(bank[4 + 2 * grp + t // 2][:], t)

        def scale_cross(out, x, k, k_neg):
            nc.scalar.activation(out=out[:, RE], in_=x[:, IM], func=COPY, scale=k_neg)
            nc.scalar.activation(out=out[:, IM], in_=x[:, RE], func=COPY, scale=k)

        def add_direct(out, x, k, addend):
            nc.vector.scalar_tensor_tensor(out=out, in0=x, scalar=k, in1=addend, op0=MULT, op1=ADD)

        def add_cross(out, x, k, k_neg):
            add_direct(out[:, RE], x[:, IM], k_neg, out[:, RE])
            add_direct(out[:, IM], x[:, RE], k, out[:, IM])

        def s0_cross(grp, t):
            scale_cross(src[grp][:, t, :], u_psum(grp, t), col(vi, grp, t), col(vi_neg, grp, t))

        def s0_half(eng, grp, t, part):
            dst, other, coef = (IM, RE, vi) if part else (RE, IM, vi_neg)
            out, x, k = src[grp][:, t, dst], u_psum(grp, t)[:, other], col(coef, grp, t)
            if eng == "S":
                nc.scalar.activation(out=out, in_=x, func=COPY, scale=k)
            else:
                nc.vector.tensor_scalar(out=out, in0=x, scalar1=k, scalar2=None, op0=MULT)

        def s0_pool(grp, t, part):
            dst, other, coef = (IM, RE, vi) if part else (RE, IM, vi_neg)
            x = slot(u_words[grp][:, t // 2, :], t)
            nc.gpsimd.tensor_scalar(out=src[grp][:, t, dst], in0=x[:, other], scalar1=col(coef, grp, t), scalar2=0.0, op0=MULT, op1=ADD)

        def a2_plain(grp, t):
            nc.scalar.activation(out=cross[grp][:, t, :], in_=bank[4 * grp + t][:], func=COPY, scale=col(wi, grp, t))

        def pack_mix(eng, grp, lo, hi):
            other = (lo + FIELDS) % WIDTH
            engines[eng].tensor_tensor(out=order_out(src_packed[grp][:, FIELDS:, :], lo, hi), in0=order_in(src[grp], lo, hi), in1=order_in(cross[grp], other, other + hi - lo), op=SUB if lo < FIELDS else ADD)

        def h_plain(grp, t):
            nc.scalar.activation(out=extra[grp][:, t, :], in_=bank[4 * grp + t][:], func=COPY, scale=col(ei, grp, t))

        def h_mix(grp, lo, hi, part):
            dst, other = (IM, RE) if part else (RE, IM)
            nc.gpsimd.tensor_tensor(out=acc[grp][:, lo:hi, dst], in0=acc[grp][:, lo:hi, dst], in1=extra[grp][:, lo:hi, other], op=ADD if part else SUB)

        def s0_direct(grp, t):
            add_direct(src[grp][:, t, :], u_psum(grp, t), col(vr, grp, t), src[grp][:, t, :])

        def keep_u(grp, u):
            nc.scalar.copy(out=u_words[grp][:, u, :], in_=bank[4 + 2 * grp + u][:])

        def order_in(x, lo, hi):
            return x[:, :, lo:hi].rearrange(PACK_IN, i=4)

        def order_out(x, lo, hi):
            return x[:, lo:hi, :].rearrange(PACK_OUT, i=4)

        def pack(eng, packed, x, lo, hi):
            move(eng, order_out(packed, lo, hi), order_in(x, lo, hi))

        def pack_src(eng, grp, lo, hi):
            pack(eng, src_packed[grp][:, FIELDS:, :], src[grp], lo, hi)

        def pack_sum(eng, grp, lo, hi):
            engines[eng].tensor_tensor(out=order_out(src_packed[grp][:, FIELDS:, :], lo, hi), in0=order_in(src[grp], lo, hi), in1=order_in(cross[grp], lo, hi), op=ADD)

        def negate(eng, grp):
            flat = src_packed[grp][:].rearrange("p x t -> p (x t)")
            out, x = flat[:, : PACK * FIELDS], flat[:, PACK * WIDTH :]
            if eng == "V":
                nc.vector.tensor_scalar(out=out, in0=x, scalar1=-1.0, scalar2=None, op0=MULT)
            elif eng == "S":
                nc.scalar.activation(out=out, in_=x, func=COPY, scale=-1.0)
            else:
                nc.gpsimd.tensor_scalar(out=out, in0=x, scalar1=-1.0, scalar2=0.0, op0=MULT, op1=ADD)

        def merge(x, grp, t):
            nc.gpsimd.tensor_tensor(out=x[grp][:, t, :], in0=x[grp][:, t, :], in1=cross[grp][:, t, :], op=ADD)

        def quantize(codes, scales, packed, lo, hi):
            flat = packed[:, lo:hi, :].rearrange("p x t -> p (x t)")
            nc.vector.quantize_mx(out=codes[:, lo:hi].bitcast(FP8X4), scales=scales[:, lo:hi], in_=flat)

        def quant_src(it, grp, lo, hi):
            quantize(src_codes[2 * it + grp], src_scales[2 * it + grp], src_packed[grp], lo, hi)

        def pack_g(eng, i, lo=0, hi=P):
            move(eng, g_packed[i][:, :, lo:hi, :].rearrange(G_OUT), g_rows[i][:, :, PACK * lo : PACK * hi].rearrange(G_IN, s=PACK))

        def pack_gs(eng, i, lo, hi):
            move(eng, g_packed[i][:, lo:hi, :, :].rearrange(G_OUT), g_rows[i][:].rearrange("p t (m s) -> p t m s", s=PACK)[:, :, :, lo:hi].rearrange(GS_IN))

        def quant_gs(i, lo, hi):
            quantize(g_codes[i], g_scales[i], g_packed[i][:].rearrange("p s m t -> p (s m) t"), P * lo, P * hi)

        def quant_g(i):
            quantize(g_codes[i], g_scales[i], g_packed[i][:].rearrange("p s m t -> p (s m) t"), 0, GROUP)

        def scatter(it, j, t, b, passes):
            for k, part in passes:
                i = chunk(part, k, j)
                cols = slice(P * t, P * (t + 1))
                window = slice(0, WIDTH) if part else slice(FIELDS, 3 * FIELDS)
                nc.tensor.matmul_mx(
                    out=bank[b][:],
                    lhsT=g_codes[i][:, cols].bitcast(FP8X4),
                    lhsT_scale=g_scales[i][:, cols],
                    rhs=src_codes[2 * it + k][:, window].bitcast(FP8X4),
                    rhs_scale=src_scales[2 * it + k][:, window],
                    start=(k, part) == (0, 0),
                    stop=(k, part) == (1, 1),
                )

        def h_scale(grp, t, b):
            scale_cross(extra[grp][:, t, :], bank[b][:], col(ei, grp, t), col(ei_neg, grp, t))

        def h_sum(grp, t):
            nc.gpsimd.tensor_tensor(out=acc[grp][:, t, :], in0=acc[grp][:, t, :], in1=extra[grp][:, t, :], op=ADD)

        def y_scale(grp, t, b):
            scale_cross(cross[grp][:, t, :], bank[b][:], col(ci, grp, t), col(ci_neg, grp, t))

        def y_sum(eng, grp, lo, hi):
            engines[eng].tensor_tensor(out=order_out(y_packed[grp], lo, hi), in0=order_in(acc[grp], lo, hi), in1=order_in(cross[grp], lo, hi), op=ADD)

        def turn_sum(grp, q, b):
            for t in range(PACK):
                for x, first in ((acc, True), (cross, False)):
                    nc.tensor.matmul(bank[b][:, P * t : P * (t + 1)], lhsT=x[grp][:, t, P * q : P * (q + 1)], rhs=ident[:], start=first, stop=not first, is_transpose=True)

        def y_half(grp, t, b, part):
            if part:
                add_direct(acc[grp][:, t, IM], bank[b][:, RE], col(ci, grp, t), acc[grp][:, t, IM])
            else:
                add_direct(acc[grp][:, t, RE], bank[b][:, IM], col(ci_neg, grp, t), acc[grp][:, t, RE])

        def store_words(grp, lo, hi):
            words = out_1[grp].rearrange("p m t -> p (m t)").bitcast(I32)
            nc.sync.dma_start(out=words[:, lo:hi], in_=y_codes[grp][:, lo:hi].bitcast(I32))

        def store_scales(eng, grp, quad):
            rows = out_2[grp, 4 * quad : 4 * quad + 4, :].bitcast(I32)
            engines[eng].dma_start(out=rows, in_=y_scales[grp][32 * quad : 32 * quad + 4, :].bitcast(I32))

        def half(out, x, k, k_neg, part, addend):
            dst, other, coef = (IM, RE, k) if part else (RE, IM, k_neg)
            if addend:
                add_direct(out[:, dst], x[:, other], coef, out[:, dst])
            else:
                nc.scalar.activation(out=out[:, dst], in_=x[:, other], func=COPY, scale=coef)

        def a2_half(grp, t, part, onto):
            half((src if onto else cross)[grp][:, t, :], bank[4 * grp + t][:], col(wi, grp, t), col(wi_neg, grp, t), part, onto)

        def h_half(grp, t, part, onto):
            half((acc if onto else extra)[grp][:, t, :], bank[4 * grp + t][:], col(ei, grp, t), col(ei_neg, grp, t), part, onto)

        def y_part(grp, t, part, onto):
            half((acc if onto else cross)[grp][:, t, :], bank[4 * grp + t][:], col(ci, grp, t), col(ci_neg, grp, t), part, onto)

        def y_half_direct(grp, t, part, onto):
            cols = IM if part else RE
            x = bank[4 * grp + t][:, cols]
            if onto:
                add_direct(acc[grp][:, t, cols], x, col(cr, grp, t), acc[grp][:, t, cols])
            else:
                nc.scalar.activation(out=src[grp][:, t, cols], in_=x, func=COPY, scale=col(cr, grp, t))

        def y_scale_direct(grp, t):
            nc.scalar.activation(out=src[grp][:, t, :], in_=bank[4 * grp + t][:], func=COPY, scale=col(cr, grp, t))

        def turn_terms(grp, q, b, terms):
            for t in range(PACK):
                for i, x in enumerate(terms):
                    nc.tensor.matmul(bank[b][:, P * t : P * (t + 1)], lhsT=x[grp][:, t, P * q : P * (q + 1)], rhs=ident[:], start=i == 0, stop=i == len(terms) - 1, is_transpose=True)

        def round_y(eng, grp, q, b):
            move(eng, y_round[grp][:, q, :].rearrange("m (p t) -> m p t", t=PACK), bank[b][:].rearrange("m (t p) -> m p t", t=PACK))

        def round_rows(eng, grp, q):
            move(eng, y_round[grp][:, q, :], y_rows[grp][:, q, :])

        def turn_back(grp, q, b):
            words = y_round[grp][:, q, :].bitcast(F32)
            for u in range(2):
                nc.tensor.transpose(bank[b][:, P * u : P * (u + 1)], words[:, u::2], ident[:])

        def words_y(eng, grp, q, b):
            words = y_packed[grp][:, P * q : P * (q + 1), :].rearrange("p m t -> p (m t)").bitcast(F32)
            move(eng, words.rearrange("p (m u) -> p m u", u=2), bank[b][:, : 2 * P].rearrange("p (u m) -> p m u", u=2))

        def a2_direct(grp, t, b):
            add_direct(src[grp][:, t, :], bank[b][:], col(wr, grp, t), src[grp][:, t, :])

        def a2_cross(grp, t, b):
            add_cross(src[grp][:, t, :], bank[b][:], col(wi, grp, t), col(wi_neg, grp, t))

        def a2_scale(grp, t, b):
            scale_cross(cross[grp][:, t, :], bank[b][:], col(wi, grp, t), col(wi_neg, grp, t))

        def h_direct(grp, t, b):
            add_direct(acc[grp][:, t, :], bank[b][:], col(er, grp, t), slot(u_words[grp][:, t // 2, :], t))

        def h_cross(grp, t, b):
            add_cross(acc[grp][:, t, :], bank[b][:], col(ei, grp, t), col(ei_neg, grp, t))

        def y_direct(grp, t, b):
            add_direct(acc[grp][:, t, :], bank[b][:], col(cr, grp, t), acc[grp][:, t, :])

        def y_cross(grp, t, b):
            add_cross(acc[grp][:, t, :], bank[b][:], col(ci, grp, t), col(ci_neg, grp, t))

        def turn_y(grp, q, b):
            for t in range(PACK):
                nc.tensor.transpose(bank[b][:, P * t : P * (t + 1)], acc[grp][:, t, P * q : P * (q + 1)], ident[:])

        def rows_y(eng, grp, q, b):
            move(eng, y_rows[grp][:, q, :].rearrange("m (p t) -> m p t", t=PACK), bank[b][:].rearrange("m (t p) -> m p t", t=PACK))

        def store_rows(grp, lo, hi):
            rows = out_0[:, :, GROUP * grp : GROUP * (grp + 1)].rearrange("c (h m) n -> m (c h) n", m=P)
            nc.sync.dma_start(out=rows[:, lo:hi, :], in_=y_rows[grp][:, lo:hi, :])

        def store_planes(grp):
            words = out_1[grp].rearrange("p m t -> p (m t)").bitcast(I32)
            nc.sync.dma_start(out=words, in_=y_codes[grp][:].bitcast(I32))
            for quad in range(4):
                rows = out_2[grp, 4 * quad : 4 * quad + 4, :].bitcast(I32)
                nc.sync.dma_start(out=rows, in_=y_scales[grp][32 * quad : 32 * quad + 4, :].bitcast(I32))

        S, V, G, Y = "S", "V", "G", "Y"
        K0, K1 = [(0, 0), (0, 1)], [(1, 0), (1, 1)]
        T4 = range(PACK)
        load_coef(v_raw, v)
        load_u_part(0, 0, 2)
        make_identity(nc, ident[:])
        load_u_part(0, 2, 4)
        load_coef(c_raw, c)
        load_g(0)
        load_u(1)
        load_g(1)
        load_g(2)
        load_g(3)
        load_g(4)
        load_g(5)
        load_g(6)
        load_g(7)
        widen(v32, vi_neg, v_raw)
        turn_u_part(0, 0, 2)
        widen(c32, ci_neg, c_raw)
        products()
        turn_u_part(0, 2, 4)
        s0_half(V, 0, 0, 0)
        pack_g(S, 0, 0, 64)
        s0_half(V, 0, 0, 1)
        turn_u(1)
        s0_half(S, 0, 1, 0)
        s0_half(S, 0, 1, 1)
        s0_half(V, 0, 2, 0)
        s0_half(V, 0, 2, 1)
        s0_half(V, 0, 3, 0)
        pack_g(V, 0, 64, 128)
        s0_half(S, 1, 0, 0)
        pack_g(V, 1, 0, 64)
        s0_half(S, 1, 0, 1)
        s0_half(S, 1, 1, 0)
        quant_g(0)
        s0_half(S, 1, 1, 1)
        s0_half(S, 1, 2, 0)
        pack_g(G, 1, 64, 128)
        s0_half(V, 0, 3, 1)
        pack_g(S, 2, 0, 64)
        s0_direct(0, 0)
        s0_half(V, 1, 2, 1)
        s0_direct(0, 1)
        s0_half(S, 1, 3, 0)
        s0_direct(0, 2)
        pack_g(S, 2, 64, 128)
        pack_g(G, 3, 0, 64)
        s0_direct(0, 3)
        s0_direct(1, 0)
        s0_half(S, 1, 3, 1)
        pack_src(S, 0, 256, 512)
        s0_direct(1, 1)
        pack_src(G, 0, 0, 256)
        s0_direct(1, 2)
        s0_direct(1, 3)
        pack_g(S, 3, 64, 128)
        negate(V, 0)
        pack_g(V, 4, 0, 64)
        pack_src(S, 1, 0, 256)
        quant_src(0, 0, FIELDS, 3 * FIELDS)
        quant_src(0, 0, 0, FIELDS)
        scatter(0, 0, 0, 0, [(0, 0)])
        quant_g(1)
        pack_g(S, 4, 64, 128)
        quant_g(2)
        scatter(0, 0, 0, 0, [(0, 1)])
        pack_src(V, 1, 256, 512)
        pack_g(S, 5, 0, 64)
        scatter(0, 0, 1, 1, [(0, 0)])
        quant_g(3)
        scatter(0, 0, 1, 1, [(0, 1)])
        scatter(0, 0, 2, 2, [(0, 0)])
        negate(V, 1)
        scatter(0, 0, 2, 2, [(0, 1)])
        quant_src(0, 1, FIELDS, 3 * FIELDS)
        pack_g(S, 5, 64, 128)
        scatter(0, 0, 3, 3, [(0, 0)])
        quant_src(0, 1, 0, FIELDS)
        scatter(0, 0, 0, 0, [(1, 0)])
        quant_g(4)
        scatter(0, 0, 0, 0, [(1, 1)])
        keep_u(0, 0)
        scatter(0, 0, 1, 1, [(1, 0)])
        quant_g(5)
        scatter(0, 0, 3, 3, [(0, 1)])
        pack_g(S, 6, 0, 64)
        scatter(0, 0, 1, 1, [(1, 1)])
        a2_direct(0, 0, 0)
        scatter(0, 1, 0, 4, [(0, 0)])
        scatter(0, 0, 2, 2, [(1, 0)])
        a2_direct(0, 1, 1)
        scatter(0, 0, 2, 2, [(1, 1)])
        scatter(0, 0, 3, 3, [(1, 0)])
        keep_u(0, 1)
        a2_half(0, 0, 1, True)
        scatter(0, 0, 3, 3, [(1, 1)])
        pack_g(G, 6, 64, 128)
        scatter(0, 1, 0, 4, [(0, 1)])
        a2_direct(0, 2, 2)
        pack_g(S, 7, 0, 64)
        scatter(0, 1, 1, 5, [(0, 0)])
        a2_direct(0, 3, 3)
        scatter(0, 1, 1, 5, [(0, 1)])
        h_direct(0, 0, 0)
        keep_u(1, 0)
        quant_g(6)
        pack_g(S, 7, 64, 128)
        scatter(0, 1, 2, 6, [(0, 0)])
        a2_half(0, 1, 1, True)
        scatter(0, 1, 0, 4, [(1, 0)])
        a2_half(0, 2, 1, True)
        scatter(0, 1, 2, 6, [(0, 1)])
        a2_half(0, 3, 1, True)
        keep_u(1, 1)
        quant_g(7)
        h_plain(0, 0)
        pack_src(G, 0, 256, 512)
        h_direct(0, 1, 1)
        scatter(0, 1, 0, 4, [(1, 1)])
        scatter(0, 1, 1, 5, [(1, 0)])
        a2_half(0, 0, 0, True)
        scatter(0, 1, 1, 5, [(1, 1)])
        h_plain(0, 1)
        a2_direct(1, 0, 4)
        scatter(0, 1, 2, 6, [(1, 0)])
        scatter(0, 1, 3, 7, [(0, 0)])
        h_plain(0, 2)
        a2_direct(1, 1, 5)
        scatter(0, 1, 3, 7, [(0, 1)])
        h_mix(0, 0, 2, 0)
        scatter(0, 1, 2, 6, [(1, 1)])
        negate(S, 0)
        a2_half(1, 0, 1, True)
        scatter(0, 1, 3, 7, [(1, 0)])
        a2_half(0, 1, 0, True)
        scatter(0, 1, 3, 7, [(1, 1)])
        a2_half(0, 2, 0, True)
        a2_half(0, 3, 0, True)
        a2_direct(1, 2, 6)
        h_mix(0, 0, 2, 1)
        pack_src(S, 0, 0, 256)
        a2_direct(1, 3, 7)
        a2_half(1, 1, 1, True)
        a2_half(1, 2, 1, True)
        h_plain(1, 0)
        a2_half(1, 3, 1, True)
        quant_src(1, 0, FIELDS, 3 * FIELDS)
        h_plain(1, 1)
        h_direct(1, 0, 4)
        pack_src(S, 1, 256, 512)
        scatter(1, 0, 0, 0, [(0, 0)])
        h_direct(1, 1, 5)
        quant_src(1, 0, 0, FIELDS)
        h_plain(1, 2)
        h_mix(1, 0, 2, 0)
        a2_half(1, 0, 0, True)
        scatter(1, 0, 0, 0, [(0, 1)])
        a2_half(1, 1, 0, True)
        negate(S, 1)
        a2_half(1, 2, 0, True)
        scatter(1, 0, 1, 1, [(0, 0)])
        a2_half(1, 3, 0, True)
        h_direct(0, 2, 2)
        scatter(1, 0, 1, 1, [(0, 1)])
        pack_src(S, 1, 0, 256)
        scatter(1, 1, 0, 4, [(0, 0)])
        h_mix(1, 0, 2, 1)
        h_direct(1, 2, 6)
        scatter(1, 1, 0, 4, [(0, 1)])
        scatter(1, 1, 1, 5, [(0, 0)])
        scatter(1, 1, 1, 5, [(0, 1)])
        h_direct(0, 3, 3)
        scatter(1, 1, 2, 6, [(0, 0)])
        scatter(1, 1, 2, 6, [(0, 1)])
        quant_src(1, 1, FIELDS, 3 * FIELDS)
        scatter(1, 0, 2, 2, [(0, 0)])
        h_plain(0, 3)
        scatter(1, 0, 2, 2, [(0, 1)])
        quant_src(1, 1, 0, FIELDS)
        scatter(1, 0, 0, 0, [(1, 0)])
        h_direct(1, 3, 7)
        h_mix(0, 2, 4, 0)
        scatter(1, 1, 0, 4, [(1, 0)])
        scatter(1, 1, 0, 4, [(1, 1)])
        scatter(1, 0, 0, 0, [(1, 1)])
        h_plain(1, 3)
        y_direct(1, 0, 4)
        scatter(1, 0, 1, 1, [(1, 0)])
        scatter(1, 0, 1, 1, [(1, 1)])
        y_part(0, 0, 0, False)
        scatter(1, 0, 3, 3, [(0, 0)])
        h_mix(0, 2, 4, 1)
        y_part(1, 0, 0, True)
        scatter(1, 0, 2, 2, [(1, 0)])
        scatter(1, 1, 1, 5, [(1, 0)])
        y_direct(0, 0, 0)
        scatter(1, 1, 1, 5, [(1, 1)])
        scatter(1, 0, 2, 2, [(1, 1)])
        y_direct(0, 1, 1)
        scatter(1, 0, 3, 3, [(0, 1)])
        y_part(0, 0, 1, False)
        scatter(1, 0, 3, 3, [(1, 0)])
        h_mix(1, 2, 4, 0)
        scatter(1, 0, 3, 3, [(1, 1)])
        y_direct(0, 2, 2)
        y_part(0, 1, 1, False)
        scatter(1, 1, 3, 7, [(0, 0)])
        y_part(0, 1, 0, False)
        scatter(1, 1, 2, 6, [(1, 0)])
        y_direct(0, 3, 3)
        scatter(1, 1, 2, 6, [(1, 1)])
        y_part(0, 2, 0, False)
        scatter(1, 1, 3, 7, [(0, 1)])
        y_part(1, 0, 1, True)
        h_mix(1, 2, 4, 1)
        y_part(0, 3, 0, False)
        turn_sum(0, 0, 0)
        y_direct(1, 1, 5)
        y_part(0, 2, 1, False)
        y_part(0, 3, 1, False)
        turn_sum(0, 1, 1)
        y_part(1, 1, 1, True)
        rows_y(S, 0, 0, 0)
        y_part(1, 1, 0, True)
        scatter(1, 1, 3, 7, [(1, 0)])
        y_sum(G, 0, 0, 128)
        rows_y(S, 0, 1, 1)
        scatter(1, 1, 3, 7, [(1, 1)])
        y_direct(1, 2, 6)
        store_rows(0, 0, 1)
        turn_sum(0, 2, 2)
        y_direct(1, 3, 7)
        store_rows(0, 1, 2)
        turn_sum(0, 3, 3)
        y_part(1, 2, 0, True)
        y_sum(G, 0, 128, 256)
        rows_y(S, 0, 2, 2)
        y_part(1, 3, 0, True)
        turn_y(1, 0, 0)
        y_part(1, 2, 1, True)
        rows_y(S, 0, 3, 3)
        store_rows(0, 2, 3)
        y_part(1, 3, 1, True)
        turn_y(1, 1, 1)
        rows_y(V, 1, 0, 0)
        turn_y(1, 2, 2)
        store_rows(0, 3, 4)
        rows_y(S, 1, 1, 1)
        turn_y(1, 3, 3)
        y_sum(V, 0, 256, 384)
        store_rows(1, 0, 1)
        rows_y(S, 1, 2, 2)
        store_rows(1, 1, 2)
        pack(V, y_packed[1], acc[1], 0, 128)
        rows_y(S, 1, 3, 3)
        y_sum(V, 0, 384, 512)
        store_rows(1, 2, 3)
        pack(S, y_packed[1], acc[1], 128, 256)
        quantize(y_codes[0], y_scales[0], y_packed[0], 0, 256)
        store_rows(1, 3, 4)
        quantize(y_codes[0], y_scales[0], y_packed[0], 256, 512)
        store_words(0, 0, 256)
        pack(V, y_packed[1], acc[1], 256, 384)
        pack(S, y_packed[1], acc[1], 384, 512)
        store_words(0, 256, 512)
        quantize(y_codes[1], y_scales[1], y_packed[1], 0, 256)
        store_scales(S, 0, 0)
        store_scales(S, 0, 1)
        store_scales(S, 0, 2)
        store_scales(S, 0, 3)
        quantize(y_codes[1], y_scales[1], y_packed[1], 256, 512)
        store_words(1, 0, 256)
        store_scales(Y, 1, 0)
        store_scales(S, 1, 1)
        store_scales(Y, 1, 2)
        store_scales(S, 1, 3)
        store_words(1, 256, 512)
